import numpy as np, ml_dtypes
CORES = [25,29,65,69,153,157,193,197]
N = 8
import mx_ref
BF = ml_dtypes.bfloat16
def gentries(a):
    return np.ascontiguousarray(a.reshape(8, 16, -1).transpose(0, 2, 1)).reshape(8, -1)
def gtable(e):
    e = np.asarray(e); return np.ascontiguousarray(e.reshape(8, -1, 16).transpose(0, 2, 1)).reshape(128, -1).astype(np.int32)
def gcols(t, e):
    v = np.concatenate([t.reshape(8, 16, -1, 4), np.zeros((8, 16, 1, 4), BF)], axis=2)
    return np.ascontiguousarray(np.stack([v[g][:, e[g]] for g in range(8)])).reshape(128, -1)
def tile(rs):
    return np.stack(rs, axis=2).reshape(128, -1).astype(BF)
def pick(q, e):
    c = np.concatenate([q[0].reshape(128, -1, 4), np.zeros((128, 1, 4), np.uint8)], axis=1); s = np.concatenate([q[1], np.ones((16, 1), np.uint8)], axis=1)
    return (np.ascontiguousarray(c[:, e].reshape(128, -1)), np.ascontiguousarray(s[:, e]))
def join(*qs):
    return (np.concatenate([q[0] for q in qs], axis=1), np.concatenate([q[1] for q in qs], axis=1))
def put(q, e, v):
    c, s = q[0].reshape(128, -1, 4).copy(), q[1].copy(); c[:, e] = v[0].reshape(128, -1, 4); s[:, e] = v[1]
    return (c.reshape(128, -1), s)
def pk(c, s):
    return (np.ascontiguousarray(c), mx_ref.live(s))
def emit(q):
    return q[0], q[1]
def packed(v, rng):
    q = [mx_ref.quantize(np.ascontiguousarray(v[r])) for r in range(N)]
    return np.stack([a for a, b in q]), np.stack([mx_ref.plane(b, rng) for a, b in q])
def values_of_codes():
    e, c = np.zeros((128, 128, 4), np.float32), np.zeros((128, 2, 4), np.uint8)
    e[np.arange(128), np.arange(128), 0] = 1
    c[:127, :, 0] = np.arange(256).reshape(2, 128).T[:127]
    return mx_ref.matmul(mx_ref.quantize(e.reshape(128, 512).astype(BF)), (c.reshape(128, 8), np.full((16, 2), 127, np.uint8))).T.reshape(-1).astype(np.float64)
CODE_VALUE, SCALE_VALUE = values_of_codes(), 2.0 ** (np.arange(256) - 127.0)
def decode(q):
    return (CODE_VALUE[q[0]].reshape(16, 8, -1, 4) * SCALE_VALUE[q[1]][:, None, :, None] + 0.0).reshape(128, -1).astype(np.float32)
def f(rng, *shape):
    return mx_ref.flush((rng.standard_normal(shape, dtype=np.float32) * np.exp2(rng.integers(-2, 3, shape[:-1] + (1,)))).astype(BF))
def wide(rng, *shape, cols=0):
    v = rng.standard_normal(shape, dtype=np.float32) * np.exp2(rng.integers(-12, 13, shape)).astype(np.float32)
    if cols: v *= np.repeat(np.exp2(rng.integers(-cols, cols + 1, shape[:-2] + (1, shape[-1] // 4))) * (rng.random(shape[:-2] + (1, shape[-1] // 4)) > 0.0625), 4, axis=-1).astype(np.float32)
    return mx_ref.flush(v.astype(BF))
T, C = 320, 128
def big(v):
    v = v.astype(np.float32)
    v[np.abs(v) < np.float32(2.0 ** -16)] = 0
    return v.astype(BF)
def numbers_of(rng):
    return {"x": np.array(f(rng, N, 128, 4 * T)), "k": np.array(f(rng, N, 128, 4 * C)), "u": np.array(f(rng, N, 128, 512)), "v": np.array(f(rng, N, 128, 512))}
def pointers(rng):
    return {"pt": np.stack([gtable(rng.integers(0, C, (8, T))) for r in range(N)]), "ad": np.stack([gtable(rng.integers(0, C, (8, C))) for r in range(N)])}
def weights(rng, still=[]):
    c = np.arange(512)
    free, hold = c[~np.isin(c // 4 % 16, still)], c[np.isin(c % 16, still)]
    m = np.zeros((N, 512, 512), np.float32)
    if len(free):
        for r in range(N): m[r, free[rng.integers(0, len(free), (12, 512))], c] = (0.5 + 1.5 * rng.random((12, 512))) * rng.choice([-1.0, 1.0], (12, 512))
    m[:, :, hold] = 0
    m[:, 4 * (hold % 128) + hold // 128, hold] = 32
    a, s = packed(m.reshape(N, 128, 4, 512).transpose(0, 1, 3, 2).reshape(N, 128, 2048).astype(BF), rng)
    return {"wc": a, "ws": s}
def setup_inputs(rng):
    return {**numbers_of(rng), **pointers(rng), **weights(rng)}
def setup_inputs_ties(rng):
    d = numbers_of(rng)
    o, e = rng.permutation(N), rng.permutation(8)
    p = rng.integers(0, C, (N, 8, T))
    for i, n in (("x", T), ("k", C)):
        a = d[i].reshape(N, 8, 16, n, 4)
        a[:, :, 0] = 0
        a[:, :, 0, :, 0] = rng.integers(0, 3, (N, 8, n)).astype(np.float32).astype(BF)
        for r in o[2:]:
            a[r, e[0], :8] = 0
            if i == "k": a[r, e[0], 0, :, 0] = 4
            else:
                w = rng.permutation(T)
                go = w // C % 2 == 1
                p[r, e[0]] = w % C
                a[r, e[0], 0, :, 0] = np.where(go, rng.integers(1, 4, T), 0).astype(np.float32).astype(BF)
                a[r, e[0], 1, :, 0] = np.where(go, 0.0, 2.0 ** 24).astype(np.float32).astype(BF)
                p[r, e[1]] = rng.integers(C)
                a[r, e[1], 0, T - 1, 0] = 3
        d[i] = a.reshape(N, 128, 4 * n)
    u = d["u"].reshape(N, 128, 128, 4)
    u[:, :, ::16] = 0
    for r in range(N):
        for h in range(0, 128, 16): u[r, h, h, 0] = 0.0 if r == o[0] else -1.0 if r == o[1] else 1.0
    d["u"] = u.reshape(N, 128, 512)
    return {**d, **pointers(rng), "pt": np.stack([gtable(p[r]) for r in range(N)]), **weights(rng, [0])}
def setup_inputs_near(rng):
    d = numbers_of(rng)
    o = rng.permutation(8)
    sign = np.where(o < 4, 1.0, -1.0)
    for i, n in (("x", T), ("k", C)):
        a = d[i].astype(np.float32).reshape(N, 8, 16, n, 4)
        a[:, :, 0] = 0
        a[:, :, 8:] = 0
        a[:, :, 0, :, 0] = sign[:, None]
        s = rng.integers(0, 16, (N, 8, n))
        a[:, :, 8] = ((s[:, :, :, None] >> np.arange(4)) & 1) * np.exp2(np.arange(4) - 23.0)
        a[:, :, 11, :, 0] = 2.0 ** -10
        for g in range(8):
            if o[g] % 4 == 2:
                a[:, g, 8:] = 0
                a[:, g, 8:10, :, 0] = rng.integers(8, 16, (N, 2, n)) * 2.0 ** -33
            if o[g] == 7:
                a[:, g, 8:] = 0
                a[:, g, 8, :, 0] = 1.96875
                a[:, g, 9, :, 0] = (1.0 + rng.random((N, n))) * np.exp2(-1.0 * rng.integers(13, 17, (N, n)))
            if o[g] % 4 == 1 and i == "x":
                for r in range(N): a[r, g, 0, rng.integers(n), 0] = sign[g] * 2.0 ** 29
        d[i] = a.reshape(N, 128, 4 * n).astype(BF)
    u = d["u"].reshape(N, 128, 128, 4)
    u[:, :, ::16] = 0
    for g in range(8):
        h, c = 16 * g, 1.0 if o[g] % 4 == 0 else 2.0 ** -30
        if o[g] % 4 < 2:
            u[:, h, h, 0] = c
            u[:, h + 11, h, 0] = c
        if o[g] % 4 == 2:
            u[:, h + 8, h, 0] = 1.125 * c
            u[:, h + 9, h, 0] = 1.25 * c if o[g] == 2 else -1.25 * c
        elif o[g] == 7: u[:, h + 9, h, 0] = 1.0
        else: u[:, h + 8, h] = c
    d["u"] = u.reshape(N, 128, 512)
    return {**d, **pointers(rng), **weights(rng, [0, 8, 9, 10, 11, 12, 13, 14, 15])}
def setup_inputs_huge(rng):
    d = numbers_of(rng)
    o = rng.permutation(N)
    for i, n in (("x", T), ("k", C)):
        a = (0.6 + 0.4 * rng.random((N, 128, n, 4))) * 2.0 ** 30
        c = rng.integers(0, 2, (N, 1, n, 1)) * 2.0 - 1.0
        c[o < N // 2] = 1
        d[i] = (a * c).astype(np.float32).reshape(N, 128, 4 * n).astype(BF)
    u = d["u"].reshape(N, 128, 128, 4)
    u[:, :, ::16] = (-2.0 ** 30 * (1 - 0.1 * rng.random((N, 128, 8, 4)))).astype(np.float32).astype(BF)
    d["u"] = u.reshape(N, 128, 512)
    return {**d, **pointers(rng), **weights(rng)}
def setup_inputs_ends(rng):
    d = numbers_of(rng)
    s, h = rng.integers(N), rng.permutation(8)
    o = np.zeros(N, int)
    o[(s - np.arange(N)) % N] = np.concatenate([[0, 2, 1], rng.permutation(np.arange(3, N))])
    e = np.concatenate([rng.permutation((s + np.arange(1, N - 1)) % N)[:2], [s, (s - 1) % N]])
    sign = rng.integers(0, 2, (8, 16, 1, 4)) * 2.0 - 1.0
    sign[h[:2]] = 1
    sign[h[2:4]] = -1
    for r in range(N):
        for i, n in (("x", T), ("k", C)):
            a = np.full((8, 16, n, 4), 2.0 ** -30)
            if o[r] % 2 == 0:
                a = 2.0 ** 30 * (1 - 0.1 * rng.random((8, 16, n, 4)))
                if o[r] == 2:
                    a *= 0.5
                    a[:, :, [0, 1 if i == "x" else C - 1]] = 2.0 ** 30
                a[h[4:6]] = 2.0 ** 30
            if o[r] == 0: a[:] = 2.0 ** 30
            d[i][r] = (a * sign).reshape(128, 4 * n).astype(np.float32).astype(BF)
        c = sign.reshape(128, 4) * (2.0 ** -30 if o[r] % 4 == 1 else 2.0 ** 30) * (-1.0 if o[r] % 4 < 2 else 1.0)
        c = c.astype(np.float32).astype(BF)
        a = d["u"][r].reshape(128, 128, 4).copy()
        a[:, ::16] = c[:, None]
        for g in h[4:6]:
            a[:, 16 * g] = 0
            a[16 * g:16 * g + 16, 16 * g] = c[16 * g:16 * g + 16]
        d["u"][r] = a.reshape(128, 512)
        if o[r] == 0: d["v"][r] = np.tile(c, (1, 128))
    p, a = rng.integers(0, C, (N, 8, T)), rng.integers(0, C, (N, 8, C))
    p[e[0]], a[e[0]] = C - 1, C - 1
    p[e[1]], a[e[1]] = 0, 0
    p[e[2]], a[e[2]] = np.arange(T) % C, np.arange(C)
    p[e[3]], a[e[3]] = (C - 1) * rng.integers(0, 2, (8, T)), C - 1 - np.arange(C)
    p[e[3], :, :4] = [0, C - 1, 0, C - 1]
    d["v"] = (np.where(d["v"] < 0, -1.0, 1.0) * np.where(rng.permutation(N) % 2, 2.0 ** -30, 2.0 ** 30)[:, None, None]).astype(np.float32).astype(BF)
    return {**d, "pt": np.stack([gtable(p[r]) for r in range(N)]), "ad": np.stack([gtable(a[r]) for r in range(N)]), **weights(rng, list(range(16)))}
def setup_inputs_spread(rng):
    d = setup_inputs(rng)
    d["x"] = big(wide(rng, N, 128, 4 * T, cols=6))
    d["k"] = big(wide(rng, N, 128, 4 * C, cols=6))
    return d
def check_inputs(d):
    b = []
    for i in ("x", "k", "u", "v"):
        a = np.abs(d[i].astype(np.float32))
        if not (np.isfinite(a).all() and ((a == 0) | (a >= 2.0 ** -30) & (a <= 2.0 ** 30)).all()): b.append("a value of " + i)
    for i in ("pt", "ad"):
        if not ((d[i] >= 0) & (d[i] < C)).all(): b.append("an entry of " + i)
    none, least, most = [emit(mx_ref.quantize(np.full((128, 16), c, np.float32).astype(BF)))[1][0, 0] for c in (0.0, 2.0 ** -30, 2.0 ** 30)]
    for r in range(N):
        if ((d["wc"][r] & 0x7F) == 0x7F).any(): b.append("wc: a code that is no number")
        s = mx_ref.live(d["ws"][r])
        if ((s != none) & ((s < least) | (s > most))).any(): b.append("ws: a scale out of range")
        a = np.abs(decode(pk(d["wc"][r], d["ws"][r])).astype(np.float64)).reshape(128, 512, 4)
        if not (np.sum(a, axis=(0, 2)) <= 32).all(): b.append("W: the sizes of a column add up to more than 32")
    return b
def half(a, b):
    return ((a.astype(np.float32) + b.astype(np.float32)) * np.float32(0.5)).astype(BF)
def parts(e):
    return np.repeat(np.repeat(e, 16, axis=0), 4, axis=1)
def inserters(s, at, n):
    g = np.arange(8)[:, None]
    o = np.argsort(-s, axis=1, kind="stable")
    place = np.zeros((8, T), np.int64)
    place[g, o] = np.arange(T)
    first = np.full((8, n), T)
    np.minimum.at(first, (np.broadcast_to(g, at.shape), at), place)
    return np.where(first < T, np.take_along_axis(o, np.minimum(first, T - 1), axis=1), -1)
def reference(x, k, u, v, pt, ad, wc, ws):
    qu = [mx_ref.quantize(u[r]) for r in range(N)]
    lay = [pk(wc[r], ws[r]) for r in range(N)]
    now = [x[r] for r in range(N)]
    cell = [decode(mx_ref.quantize(k[r])).astype(BF) for r in range(N)]
    at = [gentries(pt[r]) for r in range(N)]
    near = [gentries(ad[r]) for r in range(N)]
    for n in (C, 2 * C):
        given = []
        slot = []
        for r in range(N):
            q = mx_ref.quantize(now[r])
            own = decode(q).astype(BF)
            win = inserters(mx_ref.matmul(qu[r], q)[::16] + np.float32(0.0), at[r], n)
            a = np.where(parts(win < 0), cell[r], half(cell[r], gcols(own, win)))
            b = np.where(parts(win < 0), cell[r], half(cell[r], gcols(cell[r], near[r])))
            v0, v1 = half(own, gcols(a, at[r])), half(own, gcols(b, at[r]))
            more = mx_ref.matmul(qu[r], mx_ref.quantize(v1))[::16] > mx_ref.matmul(qu[r], mx_ref.quantize(v0))[::16]
            now[r] = np.where(parts(more), v1, v0)
            slot.append(np.where(np.take_along_axis(win, at[r], axis=1) == np.arange(T), at[r], -1))
            given.append(mx_ref.quantize(np.ascontiguousarray(a)))
            at[r] = at[r] + n * more
            near[r] = np.concatenate([np.broadcast_to(np.arange(n) + n, (8, n)), near[r]], axis=1)
            cell[r] = np.concatenate([a, b], axis=1)
        for r in range(N):
            q = given[(r - 1) % N]
            made = tile([mx_ref.matmul(pick(lay[r], np.arange(128 * b, 128 * b + 128)), q) * np.float32(0.03125) for b in range(4)])
            now[r] = np.ascontiguousarray(np.where(parts(slot[r] >= 0), gcols(made, slot[r]), now[r]))
    y, z, op = np.zeros((N, 128, T), np.float32), np.zeros((N, 128, 4 * C), np.float32), np.zeros((N, 8, T), np.float32)
    oc, osc = np.zeros((N, 128, 4 * T), np.uint8), np.zeros((N, 16, T), np.uint8)
    for r in range(N):
        q, qv = mx_ref.quantize(now[r]), mx_ref.quantize(v[r])
        y[r] = mx_ref.matmul(qv, q)
        z[r] = mx_ref.matmul(qv, mx_ref.quantize(np.ascontiguousarray(cell[r])))
        op[r] = at[r]
        oc[r], osc[r] = emit(q)
    return {"y": y, "z": z, "op": op, "oc": oc, "osc": osc}

@@ -1,0 +1,507 @@
+from concourse.bass import DstId, RemoteDMATransfer
+from concourse.mybir import dt, AluOpType as ALU, AxisListType, ActivationFunctionType as AF
+
+F4, BF, I4, U2, C8, S8 = "float32", "bfloat16", "int32", "uint16", "float8_e4m3fn_x4", "uint8"
+PL, L, LS = 576, 336, 328
+NV = 5
+NS = 20 - NV
+BIG = 2.0 ** 86
+
+
+def _sb(n, d):
+    return ("sbuf", [128, n], d)
+
+
+SCRATCH = {
+    "xs": _sb(1280, BF), "ks": _sb(512, BF), "us": _sb(512, BF), "vs": _sb(512, BF),
+    "qxk": _sb(448, C8), "sxk": _sb(448, S8), "qu": _sb(128, C8), "su": _sb(128, S8), "qur": _sb(128, C8), "sur": _sb(128, S8),
+    "qvv": _sb(128, C8), "svv": _sb(128, S8), "qw": _sb(512, C8), "sw": _sb(512, S8),
+    "et": _sb(2048, BF), "ones": _sb(128, BF), "qe": _sb(512, C8), "se": _sb(512, S8),
+    "ptw": _sb(20, I4), "ptr": _sb(320, I4), "adw": _sb(8, I4), "h16": _sb(320, I4), "lo": _sb(320, I4), "hw16": _sb(20, I4),
+    "pidx": _sb(4, I4), "cst": _sb(16, F4), "iq": _sb(320, F4), "iw": _sb(20, F4), "iw32": _sb(20, F4),
+    "clf": _sb(20, F4), "clu": _sb(20, U2), "uif": _sb(8, F4), "uiu": _sb(8, U2),
+    "vsrc": _sb(L, F4), "vk": _sb(L, F4), "kk": _sb(16, F4), "dgi": _sb(L, I4), "dg": _sb(L, F4),
+    "tb": _sb(L, F4), "hb": _sb(144, F4), "cw": _sb(16, F4), "cid": _sb(256, F4),
+    "keyr": _sb(320, F4), "keyw": _sb(20, F4), "hwf": _sb(20, F4), "junk": _sb(1920, BF), "cmpv": _sb(960, BF),
+    "acc": _sb(16, F4), "accs": _sb(2, F4), "cntv": _sb(8, F4), "posa": _sb(20, F4),
+    "plist": _sb(22, U2), "el": _sb(4, U2), "order": _sb(22, U2),
+    "vv": _sb(L, F4), "dgt": _sb(L, F4), "dgs": _sb(L, F4), "inc": _sb(LS, F4), "d0": _sb(LS, F4), "msk": _sb(320, F4),
+    "sx0": _sb(464, F4), "sx1": _sb(464, F4), "ss0": _sb(L, F4), "ss1": _sb(L, F4), "st0": _sb(L, F4), "st1": _sb(L, F4),
+    "nr0": _sb(LS, F4), "nr1": _sb(LS, F4), "s2": _sb(2 * LS, F4), "offf": _sb(16, F4), "offu": _sb(16, U2), "off2": _sb(16, F4), "offv": _sb(16, U2),
+    "fg1": _sb(4 * PL, BF), "fg2": _sb(4 * PL, BF), "gh": _sb(1536, BF), "at1": _sb(512, BF), "bt1": _sb(512, BF), "g3": _sb(2048, BF), "ab2": _sb(2048, BF),
+    "vl1": _sb(4 * 768, BF), "vl2": _sb(4 * 896, BF), "xt2": _sb(1280, BF), "xt3": _sb(1280, BF),
+    "qa1": _sb(128, C8), "sa1": _sb(128, S8), "qg": _sb(512, C8), "sg3": _sb(512, S8), "qv": _sb(640, C8), "sv3": _sb(640, S8),
+    "qx": _sb(320, C8), "sx": _sb(320, S8), "qx3": _sb(320, C8), "sx3": _sb(320, S8),
+    "adf": _sb(16, F4), "cd": _sb(16, F4), "no": _sb(16, F4), "adu": _sb(16, U2), "ptu": _sb(20, U2), "pt2f": _sb(20, F4),
+    "t0s": _sb(320, F4), "more": _sb(320, F4), "mor2": _sb(320, F4), "mw": _sb(20, F4), "sl": _sb(576, F4), "slw": _sb(20, F4), "wf": _sb(20, F4), "wu": _sb(80, U2),
+    "mm": _sb(640, F4), "pti": _sb(320, F4), "opr": _sb(640, F4), "zs": _sb(832, F4),
+    "lc1": _sb(128, C8), "ls1": _sb(128, S8), "lc2": _sb(256, C8), "ls2": _sb(256, S8),
+    "rc1": _sb(64, C8), "rs1": _sb(128, S8), "rc2": _sb(128, C8), "rs2": _sb(256, S8),
+}
+for _i in range(8):
+    SCRATCH["p%d" % _i] = ("psum", [128, 512], F4)
+_DS = ["d_ptw", "d_rep", "d_x", "d_k", "d_u", "d_v", "d_w", "d_ws", "d_ad", "d_out1", "d_out2"]
+SEMAPHORES = ["qv_s", "qs_s", "qt_s", "qg_s", "arr1", "arr2", "rin1", "rin2", "loc"] + _DS
+
+
+def _bits(es):
+    return sum(1 << e for e in es)
+
+
+def _relays(src, dst, T, topo):
+    if topo.may_write(src, dst):
+        return []
+    c = [d for d in topo.cores_of(src) if d != src and T.rank_of(d) is None and topo.may_write(d, dst)]
+    a, b = [d for d in c if topo.die(d) == topo.die(src)], [d for d in c if topo.die(d) != topo.die(src)]
+    return [d for p in zip(a, b) for d in p]
+
+
+def _hand_on(g, core, T, topo):
+    sent = 0
+    for r, src in enumerate(T.cores):
+        dst = T.cores[(r + 1) % len(T.cores)]
+        rel = _relays(src, dst, T, topo)[:3]
+        if core not in rel:
+            continue
+        j = rel.index(core)
+        es = topo.engines(core, dst)[:8]
+        rid, pid = topo.addr(dst, core)
+        for rnd, n in ((1, 128), (2, 256)):
+            g.wait_ge(T.sem["rin%d" % rnd], 8)
+            if j < 2:
+                h = n // 2
+                o, i = T["lc%d" % rnd][:, h * j:h * j + h].bitcast(dt.uint8), T["rc%d" % rnd][:, 0:h].bitcast(dt.uint8)
+            else:
+                o, i = T["ls%d" % rnd][:, 0:n], T["rs%d" % rnd][:, 0:n]
+            g.remote_dma(o, i, T.sem["arr%d" % rnd], T.sem["loc"], pid, rid, _bits(es))
+            sent += len(es)
+    if sent:
+        g.wait_ge(T.sem["loc"], sent)
+
+
+def rank_program(g, core, T, topo):
+    rank = T.rank_of(core)
+    if rank is None:
+        _hand_on(g, core, T, topo)
+        return
+    nranks = len(T.cores)
+    prev, nxt = T.cores[(rank - 1) % nranks], T.cores[(rank + 1) % nranks]
+    V, S, E, G, Y = "v", "s", "t", "g", "y"
+    eng = {V: g.vector, S: g.scalar, E: g.tensor, G: g, Y: g.sync}
+    qsem = {V: "qv_s", S: "qs_s", E: "qt_s", G: "qg_s"}
+    cnt = {V: 0, S: 0, E: 0, G: 0}
+    seen = {q: {} for q in eng}
+    hist = {}
+
+    def need(q, sem, n):
+        if seen[q].get(sem, 0) < n:
+            eng[q].wait_ge(T.sem[sem], n)
+            seen[q][sem] = n
+
+    def track(q, outs, ins, token=None):
+        acc = [(r, True) for r in outs] + [(r, False) for r in ins]
+        waits = {}
+        for (name, lo, hi, ph), w in acc:
+            ps = name[0] == "p" and name[1:].isdigit()
+            for (l2, h2, p2, w2, tok, q2) in hist.get(name, []):
+                if l2 < hi and lo < h2 and (ph is None or p2 is None or ph == p2) and (w or w2 or (ps and q2 != q)):
+                    waits[tok[0]] = max(waits.get(tok[0], 0), tok[1])
+        for s, n in waits.items():
+            need(q, s, n)
+        if token is None:
+            cnt[q] += 1
+            token = (qsem[q], cnt[q])
+        for (name, lo, hi, ph), w in acc:
+            h = hist.setdefault(name, [])
+            if w and ph is None:
+                h[:] = [e for e in h if not (lo <= e[0] and e[1] <= hi)]
+            h.append((lo, hi, ph, w, token, q))
+        return token
+
+    def run(q, outs, ins, f):
+        track(q, [o[1] for o in outs], [i[1] for i in ins])
+        f().then_inc(T.sem[qsem[q]], 1)
+
+    def A(name, lo=0, hi=None):
+        hi = SCRATCH[name][1][1] if hi is None else hi
+        return (T[name][:, lo:hi], (name, lo, hi, None))
+
+    def B4(name, lo, hi, b):
+        return (T[name][:, lo + b:hi:4], (name, lo, hi, b))
+
+    def St(name, hi, lo=15, step=16):
+        return (T[name][:, lo:hi:step], (name, 0, hi, None))
+
+    def ind(a, li):
+        return a[0] if li is None else a[0].indirect(li[0])
+
+    def opt(*xs):
+        return [x for x in xs if isinstance(x, tuple)]
+
+    def val(x):
+        return x[0] if isinstance(x, tuple) else x
+
+    def tt(o, a, b, op, li=None):
+        run(V, [o], [a, b] + opt(li), lambda: g.vector.tensor_tensor(o[0], ind(a, li), b[0], op))
+
+    def ts(o, a, s1, op0, s2=None, op1=None, li=None):
+        if op1 is None:
+            run(V, [o], [a] + opt(li, s1), lambda: g.vector.tensor_scalar(o[0], ind(a, li), val(s1), None, op0))
+        else:
+            run(V, [o], [a] + opt(li, s1, s2), lambda: g.vector.tensor_scalar(o[0], ind(a, li), val(s1), val(s2), op0, op1))
+
+    def cp(o, a, li=None):
+        run(V, [o], [a] + opt(li), lambda: g.vector.tensor_copy(o[0], ind(a, li)))
+
+    def scatter(o, li, a):
+        run(V, [o], [a, li], lambda: g.vector.tensor_copy(o[0].indirect(li[0]), a[0]))
+
+    def fill(o, c):
+        run(V, [o], [], lambda: g.vector.memset(o[0], c))
+
+    def scan(o, a, b, init, op0, op1):
+        run(V, [o], [a, b], lambda: g.vector.tensor_tensor_scan(o[0], a[0], b[0], init, op0, op1))
+
+    def act(o, a, scale=1.0, bias=0.0, func=None, li=None, accum=None):
+        fn = AF.Copy if func is None else func
+
+        def f():
+            kw = {}
+            if isinstance(bias, tuple) or bias != 0.0:
+                kw["bias"] = val(bias)
+            if scale != 1.0:
+                kw["scale"] = scale
+            if accum is not None:
+                kw["accum_out"] = accum[0]
+            return g.scalar.activation(o[0], ind(a, li), fn, **kw)
+        run(S, [o] + opt(accum), [a] + opt(li, bias), f)
+
+    def iota(o, pattern, base, cm):
+        def f():
+            if SCRATCH[o[1][0]][2] == I4:
+                return g.iota(o[0], pattern, base, cm)
+            return g.iota(o[0], pattern, base, cm, allow_small_or_imprecise_dtypes=True)
+        run(G, [o], [], f)
+
+    def quant(q, s, lo, hi, t, tlo):
+        a, b, c = A(q, lo, hi), A(s, lo, hi), A(t, tlo, tlo + 4 * (hi - lo))
+        run(V, [a, b], [c], lambda: g.vector.quantize_mx(a[0], b[0], c[0]))
+
+    def mm(p, n, wq, ws, wlo, xq, xs, xlo):
+        o = A(p, 0, n)
+        w, w2, x, x2 = A(wq, wlo, wlo + 128), A(ws, wlo, wlo + 128), A(xq, xlo, xlo + n), A(xs, xlo, xlo + n)
+        run(E, [o], [w, w2, x, x2], lambda: g.tensor.matmul_mx(o[0], w[0], w2[0], x[0], x2[0], True, True))
+
+    def dma(q, out, in_, sem, n=16, outs=(), ins=()):
+        track(q, list(outs), list(ins), token=(sem, n))
+        eng[q].dma_start(out, in_).then_inc(T.sem[sem], 16)
+
+    def load(q, name, src, sem):
+        a = A(name)
+        dma(q, a[0], src, sem, outs=[a[1]])
+
+    load(S, "ptw", T.pt[:, :], "d_ptw")
+    for q in range(16):
+        dma(S if q % 2 else Y, T.ptr[q:128:16, :], T.pt[:, :], "d_rep", n=256)
+    hist["ptr"] = [(0, 320, None, True, ("d_rep", 256), "dma")]
+    load(Y, "us", T.u[:, :], "d_u")
+    load(S, "xs", T.x[:, :], "d_x")
+    load(Y, "ks", T.k[:, :], "d_k")
+    dma(Y, T.qw[:, 0:512].bitcast(dt.uint8), T.wc[:, :], "d_w", outs=[("qw", 0, 512, None)])
+    load(Y, "sw", T.ws[:, :], "d_ws")
+    load(Y, "adw", T.ad[:, :], "d_ad")
+    load(Y, "vs", T.v[:, :], "d_v")
+
+    iota(A("pidx", 0, 1), [[1, 1]], 0, 1)
+    iota(A("iq"), [[1, 16], [16, 20]], 0, 0)
+    iota(A("iw"), [[16, 20]], 0, 0)
+    iota(A("uif"), [[16, 8]], 0, 0)
+    fill(A("ones"), 1.0)
+    fill(A("et"), 0.0)
+    for b in range(4):
+        o, i = B4("et", 512 * b, 512 * b + 512, b), A("ones")
+        run(G, [o], [i], lambda: g.affine_select(o[0], i[0], [[-1, 128]], ALU.is_equal, 0.0, 0, 1))
+    iota(A("clf"), [[1, 20]], 0, 0)
+    iota(A("vsrc", 0, 320), [[1, 320]], 0, 0)
+    iota(A("vsrc", 320, 336), [[16, 16]], 336, 0)
+    iota(A("hb"), [[1, 9], [0, 16]], 0, 0)
+    iota(A("dgi"), [[1, L]], 128, -1)
+    iota(A("tb"), [[0, 21], [1, 16]], 0, 0)
+    iota(A("kk"), [[0, 2], [16, 8]], 336, 0)
+    iota(A("cw"), [[16, 16]], 0, 0)
+    iota(A("cid"), [[1, 256]], 640, 0)
+
+    pf, q_, q8, thA, thB, addA, addB, addB2, tmpc, q20 = [A("cst", j, j + 1) for j in range(10)]
+    qi, q8i = A("pidx", 1, 2), A("pidx", 2, 3)
+    ts(qi, A("pidx", 0, 1), 15, ALU.bitwise_and)
+    ts(q8i, A("pidx", 0, 1), 7, ALU.bitwise_and)
+    cp(q_, qi)
+    cp(q8, q8i)
+    ts(A("iq"), A("iq"), 0.03125, ALU.mult)
+    ts(A("iw"), A("iw"), q_, ALU.add)
+    ts(A("iw32"), A("iw"), 0.03125, ALU.mult)
+    ts(thA, q_, 16.0, ALU.mult, 14.0, ALU.add)
+    ts(thB, q8, 16.0, ALU.mult, 14.0, ALU.add)
+    ts(tmpc, q_, 15.0, ALU.is_equal, -336.0, ALU.mult)
+    ts(addA, q_, tmpc, ALU.add, 161.0, ALU.add)
+    ts(addB, q8, 160.0, ALU.add)
+    ts(pf, q_, 8.0, ALU.is_ge, float(LS), ALU.mult)
+    tt(addB2, addB, pf, ALU.add)
+    ts(q20, q_, 20.0, ALU.mult)
+    cp(A("uiu"), A("uif"))
+
+    ts(A("h16"), A("ptr"), 0x70, ALU.bitwise_and)
+    ts(A("hw16"), A("ptw"), 0x70, ALU.bitwise_and)
+    tt(A("keyr"), A("h16"), A("iq"), ALU.add)
+    tt(A("keyw"), A("hw16"), A("iw32"), ALU.add)
+
+    def count(k, bias, out):
+        j = 320 * (k % 6)
+        act(A("junk", j, j + 320), A("keyr"), scale=-1.0, bias=bias, func=AF.Sign, accum=out)
+
+    for k in range(NS):
+        count(k, A("keyw", k, k + 1), A("acc", k, k + 1))
+    count(NS, thA, A("accs", 0, 1))
+    count(NS + 1, thB, A("accs", 1, 2))
+
+    def lane(j):
+        o, c = A("cntv", j, j + 1), A("cmpv", 320 * (j % 3), 320 * (j % 3) + 320)
+        ts(c, A("keyr"), A("keyw", NS + j, NS + j + 1), ALU.is_lt)
+        run(V, [o], [c], lambda: g.vector.tensor_reduce(o[0], c[0], AxisListType.X, ALU.add))
+
+    for j in range(2):
+        lane(j)
+    quant("qu", "su", 0, 128, "us", 0)
+    o1, i1, l1 = A("qur"), A("qu"), A("uiu")
+    run(V, [o1], [i1, l1], lambda: g.vector.tensor_copy(T.qur[:, 0:128].bitcast(dt.uint32), T.qu[:, 0:128].bitcast(dt.uint32).indirect(T.uiu[:, 0:8])))
+    cp(A("sur"), A("su"), li=l1)
+    quant("qxk", "sxk", 0, 320, "xs", 0)
+    mm("p4", 320, "qur", "sur", 0, "qxk", "sxk", 0)
+    quant("qxk", "sxk", 320, 448, "ks", 0)
+    quant("qe", "se", 0, 512, "et", 0)
+    for b in range(4):
+        mm("p%d" % b, 448, "qe", "se", 128 * b, "qxk", "sxk", 0)
+    for j in range(2, NV):
+        lane(j)
+    ts(A("clu"), A("clf"), q20, ALU.add)
+    ts(A("lo"), A("ptr"), 15, ALU.bitwise_and)
+    ts(A("msk"), A("lo"), q_, ALU.not_equal, BIG, ALU.mult, li=A("clu"))
+    ts(A("sx0", 320, 464), A("hb"), 32.0, ALU.subtract, 2.0 ** 80, ALU.mult)
+    ts(A("vk", 320, 336), A("vsrc", 320, 336), 448.0, ALU.min, q_, ALU.add)
+    ts(A("vk", 335, 336), q_, 320.0, ALU.add)
+    cp(A("vk", 0, 320), A("vsrc", 0, 320))
+    ts(A("dgi"), A("dgi"), 15, ALU.bitwise_and)
+    ts(A("dg"), A("dgi"), 0.0, ALU.not_equal, 2.0 ** 20, ALU.mult)
+    ts(A("tb"), A("tb"), 0.0, ALU.is_equal, 2.0 ** 22, ALU.mult)
+    ts(A("hwf"), A("hw16"), 0.0625, ALU.mult)
+    ts(A("kk"), A("kk"), q_, ALU.add)
+    fill(A("st0", 0, 8), 0.0)
+    fill(A("st1", 0, 8), 0.0)
+    tt(A("sx0", 0, 320), A("p4", 0, 320), A("msk"), ALU.subtract)
+    ts(A("posa", NS, 20), A("cntv", 0, NV), 1.0, ALU.add)
+    ts(A("posa", 0, NS), A("acc", 0, NS), 0.5, ALU.mult, 160.5, ALU.add)
+    tt(A("posa"), A("posa"), A("hwf"), ALU.add)
+    cp(A("plist", 0, 20), A("posa"))
+    ts(A("plist", 20, 21), A("accs", 0, 1), 0.5, ALU.mult, addA, ALU.add)
+    scatter(A("vv"), A("plist", 0, 21), A("vk"))
+
+    def diag(out, src, n):
+        tt(A("dgt", 0, n), src, A("dg", 0, n), ALU.add)
+        scan(A("dgs", 0, n), A("tb", 0, n), A("dgt", 0, n), 2.0 ** 22, ALU.max, ALU.min)
+        cp(out, St("dgs", n))
+
+    def unpack(b):
+        act(A("fg1", PL * b, PL * b + 448), A("p%d" % b, 0, 448), scale=0.5)
+        act(A("gh", 128 * b, 128 * b + 128), A("p%d" % b, 320, 448), scale=0.5)
+
+    unpack(0)
+    diag(A("order", 0, 21), A("vv"), L)
+    act(A("d0"), A("vv", 0, LS), scale=-2.0 ** 88, bias=319.5 * 2.0 ** 88, func=AF.Identity)
+    act(A("ss0"), A("sx0"), li=A("order", 0, 21))
+    for b in range(1, 4):
+        unpack(b)
+    tt(A("inc"), A("vv", 0, LS), A("vv", 1, LS + 1), ALU.subtract)
+    ts(A("el", 0, 1), A("accs", 1, 2), 0.5, ALU.mult, addB, ALU.add)
+
+    def argmax(c):
+        scan(A("st%d" % c, 8, L), A("d0"), A("ss%d" % c, 0, LS), -BIG, ALU.min, ALU.max)
+        tt(A("nr%d" % c), A("st%d" % c, 8, L), A("st%d" % c, 7, L - 1), ALU.is_equal)
+        scan(A("s2", LS * c, LS * c + LS), A("nr%d" % c), A("inc"), 0.0, ALU.mult, ALU.add)
+
+    argmax(0)
+    tt(A("offf"), A("s2", 0, LS), A("kk"), ALU.add, li=A("el", 0, 1))
+    cp(A("offu", 0, 8), A("offf", 0, 8))
+    for b in range(4):
+        f = PL * b
+        tt(B4("at1", 0, 512, b), A("fg1", f, f + 448), A("gh", 128 * b, 128 * b + 128), ALU.add, li=A("offu", 0, 8))
+    quant("qa1", "sa1", 0, 128, "at1", 0)
+
+    sent = [0]
+
+    def send(rnd, qn, sn, n):
+        for r in (A(qn, 0, n), A(sn, 0, n)):
+            track(G, [], [r[1]], token=("loc", 0))
+        lc, ls, arr, loc = T["lc%d" % rnd], T["ls%d" % rnd], T.sem["arr%d" % rnd], T.sem["loc"]
+        rel = _relays(core, nxt, T, topo)[:3]
+        if not rel:
+            es = topo.engines(core, nxt)
+            rid, pid = topo.addr(nxt, core)
+            g.remote_dma(lc[:, 0:n].bitcast(dt.uint8), T[qn][:, 0:n].bitcast(dt.uint8), arr, loc, pid, rid, _bits(es[0:8]))
+            g.remote_dma(ls[:, 0:n], T[sn][:, 0:n], arr, loc, pid, rid, _bits(es[8:16]))
+            sent[0] += 16
+        else:
+            h = n // 2
+            tr = []
+            for j in range(2):
+                rid, pid = topo.addr(rel[j], core)
+                es = topo.engines(core, rel[j])
+                tr.append(RemoteDMATransfer(dst_ids=[DstId(rid=rid, pnc=pid)], dma_engine_mask=_bits(es[8 * j:8 * j + 8]), remote_sem=T.sem["rin%d" % rnd],
+                                            src=T[qn][:, h * j:h * j + h].bitcast(dt.uint8), dst=T["rc%d" % rnd][:, 0:h].bitcast(dt.uint8)))
+            g.remote_dma_fused(tr, local_sem=loc)
+            rid, pid = topo.addr(rel[2], core)
+            g.remote_dma(T["rs%d" % rnd][:, 0:n], T[sn][:, 0:n], T.sem["rin%d" % rnd], loc, pid, rid, _bits(topo.engines(core, rel[2])[0:8]))
+            sent[0] += 24
+
+    narr = 24 if _relays(prev, core, T, topo) else 16
+    send(1, "qa1", "sa1", 128)
+
+    def parts_of_L(rnd, M, vl):
+        need(E, "arr%d" % rnd, narr)
+        for b in range(4):
+            mm("p%d" % b, M, "qw", "sw", 128 * b, "lc%d" % rnd, "ls%d" % rnd, 0)
+        for b in range(4):
+            o, i = B4(vl, 2560, 2560 + 4 * M, b), A("p%d" % b, 0, M)
+            if b % 2:
+                ts(o, i, 0.03125, ALU.mult)
+            else:
+                act(o, i, scale=0.03125)
+
+    def new_state(vl, M, xt):
+        for b in (0, 2, 1, 3):
+            o, i, li = B4(xt, 0, 1280, b), A(vl, 0, 2560 + 4 * M), A("wu", 20 * b, 20 * b + 20)
+            if b % 2:
+                act(o, i, li=li)
+            else:
+                cp(o, i, li=li)
+
+    def slots(offu, M):
+        fill(A("sl", 0, 320 + M), 0.0)
+        scatter(A("sl", 0, 320 + M), offu, A("cid", 0, M))
+        diag(A("slw"), A("sl", 0, 320), 320)
+
+    def trials(vl, fg, wa, wb, ptu):
+        for h, win in ((1, wb), (0, wa)):
+            for b in range(4):
+                tt(B4(vl, 1280 * h, 1280 * h + 1280, b), win(b), A(fg, PL * b, PL * b + 320), ALU.add, li=ptu)
+            quant("qv", "sv3", 320 * h, 320 * h + 320, vl, 1280 * h)
+            mm("p%d" % (5 + h), 320, "qur", "sur", 0, "qv", "sv3", 320 * h)
+        act(A("t0s"), A("p5", 0, 320))
+
+    def choose(more):
+        tt(A(more), A("p6", 0, 320), A("t0s"), ALU.is_gt)
+        diag(A("mw"), A(more), 320)
+        ts(A("wf"), A("mw"), 320.0, ALU.mult)
+        tt(A("wf"), A("wf"), A("iw"), ALU.add)
+        tt(A("wf"), A("wf"), A("slw"), ALU.max)
+        for b in range(4):
+            ts(A("wu", 20 * b, 20 * b + 20), A("wf"), 4.0, ALU.mult, float(b), ALU.add)
+
+    cp(A("adf", 8, 16), A("adw"))
+    ts(A("cw"), A("cw"), q_, ALU.add)
+    tt(A("cd", 0, 8), A("cw", 0, 8), A("adf", 8, 16), ALU.subtract)
+    ts(A("no", 0, 8), A("offf", 0, 8), 319.5, ALU.is_ge)
+    tt(A("no", 0, 8), A("no", 0, 8), A("cd", 0, 8), ALU.mult)
+    tt(A("no", 0, 8), A("no", 0, 8), A("adf", 8, 16), ALU.add)
+    cp(A("adu", 0, 8), A("no", 0, 8))
+    cp(A("ptu"), A("ptw"))
+    for b in range(4):
+        f = PL * b
+        tt(B4("bt1", 0, 512, b), A("gh", 128 * b, 128 * b + 128), A("fg1", f + 320, f + 448), ALU.add, li=A("adu", 0, 8))
+
+    def gh2(b, h):
+        return A("gh", 512 + 256 * b + 128 * h, 640 + 256 * b + 128 * h)
+
+    for h, t in ((1, "bt1"), (0, "at1")):
+        for b in range(4):
+            act(gh2(b, h), B4(t, 0, 512, b), scale=0.5)
+    trials("vl1", "fg1", lambda b: gh2(b, 0), lambda b: gh2(b, 1), A("ptu"))
+    slots(A("offu", 0, 8), 128)
+    choose("more")
+    act(A("mm", 0, 320), A("more"), scale=BIG)
+    act(A("mm", 320, 640), A("more"), scale=-BIG, bias=BIG, func=AF.Identity)
+    tt(A("mm", 0, 320), A("mm", 0, 320), A("msk"), ALU.add)
+    tt(A("mm", 320, 640), A("mm", 320, 640), A("msk"), ALU.add)
+    ts(A("sx1", 320, 464), A("hb"), 32.0, ALU.subtract, 2.0 ** 80, ALU.mult)
+    ts(A("el", 2, 3), A("accs", 1, 2), 0.5, ALU.mult, addB2, ALU.add)
+    for b in range(4):
+        act(A("fg2", PL * b + 320, PL * b + 576), A("gh", 512 + 256 * b, 768 + 256 * b))
+    parts_of_L(1, 128, "vl1")
+    new_state("vl1", 128, "xt2")
+    quant("qx", "sx", 0, 320, "xt2", 0)
+    mm("p4", 320, "qur", "sur", 0, "qx", "sx", 0)
+    for b in range(4):
+        mm("p%d" % b, 320, "qe", "se", 128 * b, "qx", "sx", 0)
+
+    tt(A("sx1", 0, 320), A("p4", 0, 320), A("mm", 320, 640), ALU.subtract)
+    tt(A("sx0", 0, 320), A("p4", 0, 320), A("mm", 0, 320), ALU.subtract)
+    act(A("ss1"), A("sx1"), li=A("order", 0, 21))
+    cp(A("ss0"), A("sx0"), li=A("order", 0, 21))
+    for b in range(4):
+        act(A("fg2", PL * b, PL * b + 320), A("p%d" % b, 0, 320), scale=0.5)
+    argmax(0)
+    argmax(1)
+    tt(A("off2"), A("s2"), A("kk"), ALU.add, li=A("el", 2, 3))
+    ts(A("no", 0, 8), A("off2", 8, 16), 319.5, ALU.is_ge, 128.0, ALU.mult)
+    tt(A("off2", 8, 16), A("off2", 8, 16), A("no", 0, 8), ALU.add)
+    cp(A("offv"), A("off2"))
+    for b in range(4):
+        f = PL * b
+        tt(B4("g3", 0, 1024, b), A("fg2", f, f + 576), A("gh", 512 + 256 * b, 768 + 256 * b), ALU.add, li=A("offv"))
+    quant("qg", "sg3", 0, 256, "g3", 0)
+    send(2, "qg", "sg3", 256)
+
+    ts(A("adf", 0, 8), A("cw", 0, 8), 128.0, ALU.add)
+    tt(A("cd"), A("cw"), A("adf"), ALU.subtract)
+    ts(A("no"), A("off2"), 319.5, ALU.is_ge)
+    tt(A("no"), A("no"), A("cd"), ALU.mult)
+    tt(A("no"), A("no"), A("adf"), ALU.add)
+    cp(A("adu"), A("no"))
+    ts(A("pt2f"), A("mw"), 128.0, ALU.mult)
+    tt(A("pt2f"), A("pt2f"), A("ptw"), ALU.add)
+    cp(A("ptu"), A("pt2f"))
+    for b in range(4):
+        f = PL * b
+        tt(B4("g3", 1024, 2048, b), A("gh", 512 + 256 * b, 768 + 256 * b), A("fg2", f + 320, f + 576), ALU.add, li=A("adu"))
+    for h in (1, 0):
+        for b in range(4):
+            act(A("ab2", 512 * b + 256 * h, 512 * b + 256 * h + 256), B4("g3", 1024 * h, 1024 * h + 1024, b), scale=0.5)
+    trials("vl2", "fg2", lambda b: A("ab2", 512 * b, 512 * b + 256), lambda b: A("ab2", 512 * b + 256, 512 * b + 512), A("ptu"))
+    act(A("opr", 320, 640), A("more"), scale=128.0)
+    slots(A("offv"), 256)
+    choose("mor2")
+    quant("qg", "sg3", 256, 512, "g3", 1024)
+    quant("qvv", "svv", 0, 128, "vs", 0)
+    mm("p7", 512, "qvv", "svv", 0, "qg", "sg3", 0)
+    act(A("zs", 0, 512), A("p7"))
+    dma(Y, T.z[:, :], T.zs[:, 0:512], "d_out1", ins=[A("zs", 0, 512)[1]])
+    cp(A("pti"), A("ptr"), li=A("clu"))
+    tt(A("opr", 0, 320), A("opr", 320, 640), A("pti"), ALU.add)
+    act(A("pti"), A("mor2"), scale=256.0)
+    tt(A("opr", 0, 320), A("opr", 0, 320), A("pti"), ALU.add)
+    dma(Y, T.op[:, :], T.opr[0:128:16, 0:320], "d_out1", ins=[A("opr", 0, 320)[1]])
+
+    parts_of_L(2, 256, "vl2")
+    new_state("vl2", 256, "xt3")
+    quant("qx3", "sx3", 0, 320, "xt3", 0)
+    mm("p4", 320, "qvv", "svv", 0, "qx3", "sx3", 0)
+    dma(Y, T.oc[:, :], T.qx3[:, 0:320].bitcast(dt.uint8), "d_out1", ins=[A("qx3")[1]])
+    for k in range(4):
+        dma(Y, T.osc[4 * k:4 * k + 4, :], T.sx3[32 * k:32 * k + 4, 0:320], "d_out1", ins=[A("sx3")[1]])
+    act(A("zs", 512, 832), A("p4", 0, 320))
+    dma(S, T.y[:, :], T.zs[:, 512:832], "d_out2", ins=[A("zs", 512, 832)[1]])
+
+    for q in (V, S, E, G):
+        need(G, qsem[q], cnt[q])
+    for s, n in (("d_ptw", 16), ("d_rep", 256), ("d_x", 16), ("d_k", 16), ("d_u", 16), ("d_v", 16), ("d_w", 16), ("d_ws", 16), ("d_ad", 16), ("d_out1", 112), ("d_out2", 16),
+                 ("loc", sent[0]), ("arr1", narr), ("arr2", narr)):
+        need(G, s, n)

@@ -18,30 +18,38 @@ SCRATCH = {
     "qvv": _sb(128, C8), "svv": _sb(128, S8), "qw": _sb(512, C8), "sw": _sb(512, S8),
     "et": _sb(2048, BF), "ones": _sb(128, BF), "qe": _sb(512, C8), "se": _sb(512, S8),
     "ptw": _sb(20, I4), "ptr": _sb(320, I4), "adw": _sb(8, I4), "h16": _sb(320, I4), "lo": _sb(320, I4), "hw16": _sb(20, I4),
-    "pidx": _sb(4, I4), "cst": _sb(16, F4), "iq": _sb(320, F4), "iw": _sb(20, F4), "iw32": _sb(20, F4),
-    "clf": _sb(20, F4), "clu": _sb(20, U2), "uif": _sb(8, F4), "uiu": _sb(8, U2),
-    "vsrc": _sb(L, F4), "vk": _sb(L, F4), "kk": _sb(16, F4), "dgi": _sb(L, I4), "dg": _sb(L, F4),
-    "tb": _sb(L, F4), "hb": _sb(144, F4), "cw": _sb(16, F4), "cid": _sb(256, F4),
-    "keyr": _sb(320, F4), "keyw": _sb(20, F4), "hwf": _sb(20, F4), "junk": _sb(1920, BF), "cmpv": _sb(960, BF),
-    "acc": _sb(16, F4), "accs": _sb(2, F4), "cntv": _sb(8, F4), "posa": _sb(20, F4),
-    "plist": _sb(22, U2), "el": _sb(4, U2), "order": _sb(22, U2),
-    "vv": _sb(L, F4), "dgt": _sb(L, F4), "dgs": _sb(L, F4), "inc": _sb(LS, F4), "d0": _sb(LS, F4), "msk": _sb(320, F4),
-    "sx0": _sb(464, F4), "sx1": _sb(464, F4), "ss0": _sb(L, F4), "ss1": _sb(L, F4), "st0": _sb(L, F4), "st1": _sb(L, F4),
-    "nr0": _sb(LS, F4), "nr1": _sb(LS, F4), "s2": _sb(2 * LS, F4), "offf": _sb(16, F4), "offu": _sb(16, U2), "off2": _sb(16, F4), "offv": _sb(16, U2),
+    "pidx": _sb(4, I4), "dgi": _sb(16, I4), "iq": _sb(320, F4), "vk": _sb(L, F4), "dg": _sb(L, F4), "tb": _sb(L, F4), "hb": _sb(144, F4), "cid": _sb(256, F4),
+    "keyr": _sb(320, F4), "junk": _sb(1920, BF), "cmpv": _sb(960, BF),
+    "vv": _sb(L, F4), "dgt": _sb(L, F4), "dgs": _sb(L, F4), "inc": _sb(LS, F4), "d0": _sb(LS, F4), "msk": _sb(320, F4), "mks": _sb(2 * L, F4),
+    "sx0": _sb(464, F4), "ss0": _sb(L, F4), "ss1": _sb(L, F4), "st0": _sb(L, F4), "st1": _sb(L, F4),
+    "nr0": _sb(LS, F4), "nr1": _sb(LS, F4), "s2": _sb(2 * LS, F4), "offu": _sb(16, U2),
     "fg1": _sb(4 * PL, BF), "fg2": _sb(4 * PL, BF), "gh": _sb(1536, BF), "at1": _sb(512, BF), "bt1": _sb(512, BF), "g3": _sb(2048, BF), "ab2": _sb(2048, BF),
-    "vl1": _sb(4 * 768, BF), "vl2": _sb(4 * 896, BF), "xt2": _sb(1280, BF), "xt3": _sb(1280, BF),
-    "qa1": _sb(128, C8), "sa1": _sb(128, S8), "qg": _sb(512, C8), "sg3": _sb(512, S8), "qv": _sb(640, C8), "sv3": _sb(640, S8),
+    "vl1": _sb(4 * 768, BF), "vl2": _sb(4 * 896, BF), "xt2": _sb(1280, BF), "xt3": _sb(1280, BF), "fgx": _sb(1792, BF), "ghx": _sb(512, BF), "atx": _sb(512, BF),
+    "tv1": _sb(2560, BF), "tv2": _sb(2560, BF),
+    "qa1": _sb(128, C8), "sa1": _sb(128, S8), "qax": _sb(128, C8), "sax": _sb(128, S8), "qg": _sb(512, C8), "sg3": _sb(512, S8), "qv": _sb(640, C8), "sv3": _sb(640, S8),
     "qx": _sb(320, C8), "sx": _sb(320, S8), "qx3": _sb(320, C8), "sx3": _sb(320, S8),
-    "adf": _sb(16, F4), "cd": _sb(16, F4), "no": _sb(16, F4), "adu": _sb(16, U2), "ptu": _sb(20, U2), "pt2f": _sb(20, F4),
-    "t0s": _sb(320, F4), "more": _sb(320, F4), "mor2": _sb(320, F4), "mw": _sb(20, F4), "sl": _sb(576, F4), "slw": _sb(20, F4), "wf": _sb(20, F4), "wu": _sb(80, U2),
-    "mm": _sb(640, F4), "pti": _sb(320, F4), "opr": _sb(640, F4), "zs": _sb(832, F4),
-    "lc1": _sb(128, C8), "ls1": _sb(128, S8), "lc2": _sb(256, C8), "ls2": _sb(256, S8),
-    "rc1": _sb(64, C8), "rs1": _sb(128, S8), "rc2": _sb(128, C8), "rs2": _sb(256, S8),
+    "t0s": _sb(320, F4), "more": _sb(464, F4), "mor2": _sb(320, F4), "sl": _sb(576, F4), "pti": _sb(320, F4), "opr": _sb(640, F4), "zs": _sb(832, F4),
+    "lcx": _sb(448, C8), "lsx": _sb(448, S8), "llx": _sb(8, U2), "lc1": _sb(128, C8), "ls1": _sb(128, S8), "lc2": _sb(256, C8), "ls2": _sb(256, S8),
+    "rcx": _sb(224, C8), "rsx": _sb(448, S8), "rlx": _sb(8, U2), "rc2": _sb(128, C8), "rs2": _sb(256, S8),
 }
+ALIAS = {}
+
+
+def _pack(base, dtype, parts):
+    at = 0
+    for n, w in parts:
+        ALIAS[n] = (base, at, w)
+        at += -(-w // 16) * 16
+    SCRATCH[base] = _sb(at, dtype)
+
+
+_pack("sm", F4, [("cst", 16), ("iw", 20), ("iw32", 20), ("clf", 22), ("uif", 8), ("vsrc", 16), ("kk", 16), ("cw", 16), ("dg16", 16), ("keyw", 20), ("hwf", 20), ("acc", 16), ("accs", 2),
+                 ("cntv", 8), ("posa", 20), ("offf", 16), ("off2", 16), ("adf", 16), ("cd", 16), ("no", 16), ("pt2f", 20), ("mw", 20), ("slw", 20), ("wf", 20)])
+_pack("ul", U2, [("clu", 20), ("uiu", 8), ("dgl", 22), ("plist", 22), ("el", 4), ("order", 22), ("offv", 16), ("adu", 16), ("ptu", 20), ("wu", 80)])
 for _i in range(8):
     SCRATCH["p%d" % _i] = ("psum", [128, 512], F4)
 _DS = ["d_ptw", "d_rep", "d_x", "d_k", "d_u", "d_v", "d_w", "d_ws", "d_ad", "d_out1", "d_out2"]
-SEMAPHORES = ["qv_s", "qs_s", "qt_s", "qg_s", "arr1", "arr2", "rin1", "rin2", "loc"] + _DS
+SEMAPHORES = ["qv_s", "qs_s", "qt_s", "qg_s", "arr1", "arr2", "arrx", "arrl", "rinx", "rinl", "rin2", "loc"] + _DS
 
 
 def _bits(es):
@@ -53,28 +61,35 @@ def _relays(src, dst, T, topo):
         return []
     c = [d for d in topo.cores_of(src) if d != src and T.rank_of(d) is None and topo.may_write(d, dst)]
     a, b = [d for d in c if topo.die(d) == topo.die(src)], [d for d in c if topo.die(d) != topo.die(src)]
-    return [d for p in zip(a, b) for d in p]
+    return [d for p in zip(a, b) for d in p][:3]
 
 
 def _hand_on(g, core, T, topo):
     sent = 0
     for r, src in enumerate(T.cores):
         dst = T.cores[(r + 1) % len(T.cores)]
-        rel = _relays(src, dst, T, topo)[:3]
+        rel = _relays(src, dst, T, topo)
         if core not in rel:
             continue
         j = rel.index(core)
-        es = topo.engines(core, dst)[:8]
         rid, pid = topo.addr(dst, core)
-        for rnd, n in ((1, 128), (2, 256)):
-            g.wait_ge(T.sem["rin%d" % rnd], 8)
+        m = _bits(topo.engines(core, dst)[:8])
+
+        def piece(tag, n):
+            g.wait_ge(T.sem["rin" + tag], 8)
             if j < 2:
                 h = n // 2
-                o, i = T["lc%d" % rnd][:, h * j:h * j + h].bitcast(dt.uint8), T["rc%d" % rnd][:, 0:h].bitcast(dt.uint8)
+                o, i = T["lc" + tag][:, h * j:h * j + h].bitcast(dt.uint8), T["rc" + tag][:, 0:h].bitcast(dt.uint8)
             else:
-                o, i = T["ls%d" % rnd][:, 0:n], T["rs%d" % rnd][:, 0:n]
-            g.remote_dma(o, i, T.sem["arr%d" % rnd], T.sem["loc"], pid, rid, _bits(es))
-            sent += len(es)
+                o, i = T["ls" + tag][:, 0:n], T["rs" + tag][:, 0:n]
+            g.remote_dma(o, i, T.sem["arr" + tag], T.sem["loc"], pid, rid, m)
+        piece("x", 448)
+        if j == 2:
+            g.wait_ge(T.sem["rinl"], 8)
+            g.remote_dma(T.llx[:, 0:8], T.rlx[:, 0:8], T.sem["arrl"], T.sem["loc"], pid, rid, m)
+            sent += 8
+        piece("2", 256)
+        sent += 16
     if sent:
         g.wait_ge(T.sem["loc"], sent)
 
@@ -86,6 +101,7 @@ def rank_program(g, core, T, topo):
         return
     nranks = len(T.cores)
     prev, nxt = T.cores[(rank - 1) % nranks], T.cores[(rank + 1) % nranks]
+    rel, far = _relays(core, nxt, T, topo), bool(_relays(prev, core, T, topo))
     V, S, E, G, Y = "v", "s", "t", "g", "y"
     eng = {V: g.vector, S: g.scalar, E: g.tensor, G: g, Y: g.sync}
     qsem = {V: "qv_s", S: "qs_s", E: "qt_s", G: "qg_s"}
@@ -123,6 +139,9 @@ def rank_program(g, core, T, topo):
         f().then_inc(T.sem[qsem[q]], 1)
 
     def A(name, lo=0, hi=None):
+        if name in ALIAS:
+            name, at, w = ALIAS[name]
+            lo, hi = at + lo, at + (w if hi is None else hi)
         hi = SCRATCH[name][1][1] if hi is None else hi
         return (T[name][:, lo:hi], (name, lo, hi, None))
 
@@ -200,6 +219,32 @@ def rank_program(g, core, T, topo):
         a = A(name)
         dma(q, a[0], src, sem, outs=[a[1]])
 
+    sent = [0]
+
+    def remote(out, src, reg, sem, dst, es):
+        track(G, [], [reg], token=("loc", 0))
+        rid, pid = topo.addr(dst, core)
+        g.remote_dma(out, src, T.sem[sem], T.sem["loc"], pid, rid, _bits(es))
+        sent[0] += len(es)
+
+    def send(tag, qn, sn, n):
+        c, s = A(qn, 0, n), A(sn, 0, n)
+        if not rel:
+            es = topo.engines(core, nxt)
+            remote(T["lc" + tag][:, 0:n].bitcast(dt.uint8), c[0].bitcast(dt.uint8), c[1], "arr" + tag, nxt, es[0:8])
+            remote(T["ls" + tag][:, 0:n], s[0], s[1], "arr" + tag, nxt, es[8:16])
+            return
+        track(G, [], [c[1]], token=("loc", 0))
+        h, tr = n // 2, []
+        for j in range(2):
+            rid, pid = topo.addr(rel[j], core)
+            es = topo.engines(core, rel[j])[8 * j:8 * j + 8]
+            tr.append(RemoteDMATransfer(dst_ids=[DstId(rid=rid, pnc=pid)], dma_engine_mask=_bits(es), remote_sem=T.sem["rin" + tag],
+                                        src=T[qn][:, h * j:h * j + h].bitcast(dt.uint8), dst=T["rc" + tag][:, 0:h].bitcast(dt.uint8)))
+            sent[0] += len(es)
+        g.remote_dma_fused(tr, local_sem=T.sem["loc"])
+        remote(T["rs" + tag][:, 0:n], s[0], s[1], "rin" + tag, rel[2], topo.engines(core, rel[2])[0:8])
+
     load(S, "ptw", T.pt[:, :], "d_ptw")
     for q in range(16):
         dma(S if q % 2 else Y, T.ptr[q:128:16, :], T.pt[:, :], "d_rep", n=256)
@@ -215,29 +260,34 @@ def rank_program(g, core, T, topo):
     iota(A("pidx", 0, 1), [[1, 1]], 0, 1)
     iota(A("iq"), [[1, 16], [16, 20]], 0, 0)
     iota(A("iw"), [[16, 20]], 0, 0)
+    iota(A("clf"), [[1, 22]], 0, 0)
+    iota(A("dgi"), [[1, 16]], 128, -1)
     iota(A("uif"), [[16, 8]], 0, 0)
-    fill(A("ones"), 1.0)
+    iota(A("kk"), [[0, 2], [16, 8]], 336, 0)
+    iota(A("hb"), [[1, 9], [0, 16]], 0, 0)
+    fill(A("ones"), 0.5)
     fill(A("et"), 0.0)
     for b in range(4):
         o, i = B4("et", 512 * b, 512 * b + 512, b), A("ones")
         run(G, [o], [i], lambda: g.affine_select(o[0], i[0], [[-1, 128]], ALU.is_equal, 0.0, 0, 1))
-    iota(A("clf"), [[1, 20]], 0, 0)
-    iota(A("vsrc", 0, 320), [[1, 320]], 0, 0)
-    iota(A("vsrc", 320, 336), [[16, 16]], 336, 0)
-    iota(A("hb"), [[1, 9], [0, 16]], 0, 0)
-    iota(A("dgi"), [[1, L]], 128, -1)
-    iota(A("tb"), [[0, 21], [1, 16]], 0, 0)
-    iota(A("kk"), [[0, 2], [16, 8]], 336, 0)
+    iota(A("vk", 0, 320), [[1, 320]], 0, 0)
+    iota(A("vsrc"), [[16, 16]], 336, 0)
+    iota(A("tb"), [[0, L]], 0, 0)
+    iota(St("tb", L, 0), [[0, 21]], 2 ** 22, 0)
+    iota(A("st0", 0, 8), [[0, 8]], 0, 0)
+    iota(A("st1", 0, 8), [[0, 8]], 0, 0)
     iota(A("cw"), [[16, 16]], 0, 0)
-    iota(A("cid"), [[1, 256]], 640, 0)
 
     pf, q_, q8, thA, thB, addA, addB, addB2, tmpc, q20 = [A("cst", j, j + 1) for j in range(10)]
     qi, q8i = A("pidx", 1, 2), A("pidx", 2, 3)
+    act(A("iq"), A("iq"), scale=0.03125)
     ts(qi, A("pidx", 0, 1), 15, ALU.bitwise_and)
     ts(q8i, A("pidx", 0, 1), 7, ALU.bitwise_and)
     cp(q_, qi)
     cp(q8, q8i)
-    ts(A("iq"), A("iq"), 0.03125, ALU.mult)
+    ts(A("dgl"), A("clf"), 0.0, ALU.mult, q_, ALU.add)
+    ts(A("dgi"), A("dgi"), 15, ALU.bitwise_and)
+    ts(A("dg16"), A("dgi"), 0.0, ALU.not_equal, 2.0 ** 20, ALU.mult)
     ts(A("iw"), A("iw"), q_, ALU.add)
     ts(A("iw32"), A("iw"), 0.03125, ALU.mult)
     ts(thA, q_, 16.0, ALU.mult, 14.0, ALU.add)
@@ -249,6 +299,11 @@ def rank_program(g, core, T, topo):
     tt(addB2, addB, pf, ALU.add)
     ts(q20, q_, 20.0, ALU.mult)
     cp(A("uiu"), A("uif"))
+    ts(A("clu"), A("clf", 0, 20), q20, ALU.add)
+    act(A("dg"), A("dg16"), li=A("dgl", 0, 21))
+    act(A("kk"), A("kk"), bias=q_, func=AF.Identity)
+    act(A("sx0", 320, 464), A("hb"), scale=2.0 ** 80, bias=-32 * 2.0 ** 80, func=AF.Identity)
+    act(A("more", 320, 464), A("hb"), scale=0.0, bias=0.5, func=AF.Identity)
 
     ts(A("h16"), A("ptr"), 0x70, ALU.bitwise_and)
     ts(A("hw16"), A("ptw"), 0x70, ALU.bitwise_and)
@@ -262,41 +317,35 @@ def rank_program(g, core, T, topo):
     for k in range(NS):
         count(k, A("keyw", k, k + 1), A("acc", k, k + 1))
     count(NS, thA, A("accs", 0, 1))
-    count(NS + 1, thB, A("accs", 1, 2))
 
     def lane(j):
         o, c = A("cntv", j, j + 1), A("cmpv", 320 * (j % 3), 320 * (j % 3) + 320)
         ts(c, A("keyr"), A("keyw", NS + j, NS + j + 1), ALU.is_lt)
         run(V, [o], [c], lambda: g.vector.tensor_reduce(o[0], c[0], AxisListType.X, ALU.add))
 
-    for j in range(2):
-        lane(j)
+    lane(0)
+    lane(1)
+    quant("qxk", "sxk", 0, 320, "xs", 0)
+    quant("qxk", "sxk", 320, 448, "ks", 0)
+    if rel:
+        send("x", "qxk", "sxk", 448)
+    iota(A("cid"), [[1, 256]], 640, 0)
+    iota(A("sl", 0, 448), [[0, 448]], 0, 0)
     quant("qu", "su", 0, 128, "us", 0)
     o1, i1, l1 = A("qur"), A("qu"), A("uiu")
-    run(V, [o1], [i1, l1], lambda: g.vector.tensor_copy(T.qur[:, 0:128].bitcast(dt.uint32), T.qu[:, 0:128].bitcast(dt.uint32).indirect(T.uiu[:, 0:8])))
+    run(V, [o1], [i1, l1], lambda: g.vector.tensor_copy(T.qur[:, 0:128].bitcast(dt.uint32), T.qu[:, 0:128].bitcast(dt.uint32).indirect(l1[0])))
     cp(A("sur"), A("su"), li=l1)
-    quant("qxk", "sxk", 0, 320, "xs", 0)
     mm("p4", 320, "qur", "sur", 0, "qxk", "sxk", 0)
-    quant("qxk", "sxk", 320, 448, "ks", 0)
     quant("qe", "se", 0, 512, "et", 0)
     for b in range(4):
         mm("p%d" % b, 448, "qe", "se", 128 * b, "qxk", "sxk", 0)
     for j in range(2, NV):
         lane(j)
-    ts(A("clu"), A("clf"), q20, ALU.add)
     ts(A("lo"), A("ptr"), 15, ALU.bitwise_and)
     ts(A("msk"), A("lo"), q_, ALU.not_equal, BIG, ALU.mult, li=A("clu"))
-    ts(A("sx0", 320, 464), A("hb"), 32.0, ALU.subtract, 2.0 ** 80, ALU.mult)
-    ts(A("vk", 320, 336), A("vsrc", 320, 336), 448.0, ALU.min, q_, ALU.add)
+    ts(A("vk", 320, 336), A("vsrc"), 448.0, ALU.min, q_, ALU.add)
     ts(A("vk", 335, 336), q_, 320.0, ALU.add)
-    cp(A("vk", 0, 320), A("vsrc", 0, 320))
-    ts(A("dgi"), A("dgi"), 15, ALU.bitwise_and)
-    ts(A("dg"), A("dgi"), 0.0, ALU.not_equal, 2.0 ** 20, ALU.mult)
-    ts(A("tb"), A("tb"), 0.0, ALU.is_equal, 2.0 ** 22, ALU.mult)
     ts(A("hwf"), A("hw16"), 0.0625, ALU.mult)
-    ts(A("kk"), A("kk"), q_, ALU.add)
-    fill(A("st0", 0, 8), 0.0)
-    fill(A("st1", 0, 8), 0.0)
     tt(A("sx0", 0, 320), A("p4", 0, 320), A("msk"), ALU.subtract)
     ts(A("posa", NS, 20), A("cntv", 0, NV), 1.0, ALU.add)
     ts(A("posa", 0, NS), A("acc", 0, NS), 0.5, ALU.mult, 160.5, ALU.add)
@@ -310,18 +359,19 @@ def rank_program(g, core, T, topo):
         scan(A("dgs", 0, n), A("tb", 0, n), A("dgt", 0, n), 2.0 ** 22, ALU.max, ALU.min)
         cp(out, St("dgs", n))
 
-    def unpack(b):
-        act(A("fg1", PL * b, PL * b + 448), A("p%d" % b, 0, 448), scale=0.5)
-        act(A("gh", 128 * b, 128 * b + 128), A("p%d" % b, 320, 448), scale=0.5)
+    def unpack(b, fg, w, gh):
+        act(A(fg, w * b, w * b + 448), A("p%d" % b, 0, 448))
+        act(A(gh, 128 * b, 128 * b + 128), A("p%d" % b, 320, 448))
 
-    unpack(0)
+    unpack(0, "fg1", PL, "gh")
+    unpack(1, "fg1", PL, "gh")
     diag(A("order", 0, 21), A("vv"), L)
     act(A("d0"), A("vv", 0, LS), scale=-2.0 ** 88, bias=319.5 * 2.0 ** 88, func=AF.Identity)
     act(A("ss0"), A("sx0"), li=A("order", 0, 21))
-    for b in range(1, 4):
-        unpack(b)
+    for b in range(2, 4):
+        unpack(b, "fg1", PL, "gh")
     tt(A("inc"), A("vv", 0, LS), A("vv", 1, LS + 1), ALU.subtract)
-    ts(A("el", 0, 1), A("accs", 1, 2), 0.5, ALU.mult, addB, ALU.add)
+    ts(A("el", 0, 1), A("accs", 0, 1), 0.5, ALU.mult, addB, ALU.add)
 
     def argmax(c):
         scan(A("st%d" % c, 8, L), A("d0"), A("ss%d" % c, 0, LS), -BIG, ALU.min, ALU.max)
@@ -331,44 +381,19 @@ def rank_program(g, core, T, topo):
     argmax(0)
     tt(A("offf"), A("s2", 0, LS), A("kk"), ALU.add, li=A("el", 0, 1))
     cp(A("offu", 0, 8), A("offf", 0, 8))
+    if rel:
+        r = A("offu", 0, 8)
+        remote(T.rlx[:, 0:8], r[0], r[1], "rinl", rel[2], topo.engines(core, rel[2])[0:8])
     for b in range(4):
         f = PL * b
         tt(B4("at1", 0, 512, b), A("fg1", f, f + 448), A("gh", 128 * b, 128 * b + 128), ALU.add, li=A("offu", 0, 8))
-    quant("qa1", "sa1", 0, 128, "at1", 0)
+    if not rel:
+        quant("qa1", "sa1", 0, 128, "at1", 0)
+        send("1", "qa1", "sa1", 128)
 
-    sent = [0]
-
-    def send(rnd, qn, sn, n):
-        for r in (A(qn, 0, n), A(sn, 0, n)):
-            track(G, [], [r[1]], token=("loc", 0))
-        lc, ls, arr, loc = T["lc%d" % rnd], T["ls%d" % rnd], T.sem["arr%d" % rnd], T.sem["loc"]
-        rel = _relays(core, nxt, T, topo)[:3]
-        if not rel:
-            es = topo.engines(core, nxt)
-            rid, pid = topo.addr(nxt, core)
-            g.remote_dma(lc[:, 0:n].bitcast(dt.uint8), T[qn][:, 0:n].bitcast(dt.uint8), arr, loc, pid, rid, _bits(es[0:8]))
-            g.remote_dma(ls[:, 0:n], T[sn][:, 0:n], arr, loc, pid, rid, _bits(es[8:16]))
-            sent[0] += 16
-        else:
-            h = n // 2
-            tr = []
-            for j in range(2):
-                rid, pid = topo.addr(rel[j], core)
-                es = topo.engines(core, rel[j])
-                tr.append(RemoteDMATransfer(dst_ids=[DstId(rid=rid, pnc=pid)], dma_engine_mask=_bits(es[8 * j:8 * j + 8]), remote_sem=T.sem["rin%d" % rnd],
-                                            src=T[qn][:, h * j:h * j + h].bitcast(dt.uint8), dst=T["rc%d" % rnd][:, 0:h].bitcast(dt.uint8)))
-            g.remote_dma_fused(tr, local_sem=loc)
-            rid, pid = topo.addr(rel[2], core)
-            g.remote_dma(T["rs%d" % rnd][:, 0:n], T[sn][:, 0:n], T.sem["rin%d" % rnd], loc, pid, rid, _bits(topo.engines(core, rel[2])[0:8]))
-            sent[0] += 24
-
-    narr = 24 if _relays(prev, core, T, topo) else 16
-    send(1, "qa1", "sa1", 128)
-
-    def parts_of_L(rnd, M, vl):
-        need(E, "arr%d" % rnd, narr)
+    def parts_of_L(qn, sn, M, vl):
         for b in range(4):
-            mm("p%d" % b, M, "qw", "sw", 128 * b, "lc%d" % rnd, "ls%d" % rnd, 0)
+            mm("p%d" % b, M, "qw", "sw", 128 * b, qn, sn, 0)
         for b in range(4):
             o, i = B4(vl, 2560, 2560 + 4 * M, b), A("p%d" % b, 0, M)
             if b % 2:
@@ -385,27 +410,41 @@ def rank_program(g, core, T, topo):
                 cp(o, i, li=li)
 
     def slots(offu, M):
-        fill(A("sl", 0, 320 + M), 0.0)
         scatter(A("sl", 0, 320 + M), offu, A("cid", 0, M))
         diag(A("slw"), A("sl", 0, 320), 320)
 
-    def trials(vl, fg, wa, wb, ptu):
-        for h, win in ((1, wb), (0, wa)):
-            for b in range(4):
-                tt(B4(vl, 1280 * h, 1280 * h + 1280, b), win(b), A(fg, PL * b, PL * b + 320), ALU.add, li=ptu)
-            quant("qv", "sv3", 320 * h, 320 * h + 320, vl, 1280 * h)
-            mm("p%d" % (5 + h), 320, "qur", "sur", 0, "qv", "sv3", 320 * h)
-        act(A("t0s"), A("p5", 0, 320))
+    own = (1, 2)
+
+    def picks(h, tv, win):
+        for b in range(own[h], 4):
+            act(A(tv, 1280 * h + 320 * b, 1280 * h + 320 * b + 320), win(b), li=A("ptu"))
+
+    def trial(h, vl, fg, tv, win):
+        for b in range(4):
+            o = B4(vl, 1280 * h, 1280 * h + 1280, b)
+            if b < own[h]:
+                tt(o, win(b), A(fg, PL * b, PL * b + 320), ALU.add, li=A("ptu"))
+            else:
+                tt(o, A("p%d" % b, 0, 320), A(tv, 1280 * h + 320 * b, 1280 * h + 320 * b + 320), ALU.add)
+        quant("qv", "sv3", 320 * h, 320 * h + 320, vl, 1280 * h)
+        mm("p%d" % (5 + h), 320, "qur", "sur", 0, "qv", "sv3", 320 * h)
 
     def choose(more):
-        tt(A(more), A("p6", 0, 320), A("t0s"), ALU.is_gt)
-        diag(A("mw"), A(more), 320)
+        tt(A(more, 0, 320), A("p6", 0, 320), A("t0s"), ALU.is_gt)
+        diag(A("mw"), A(more, 0, 320), 320)
         ts(A("wf"), A("mw"), 320.0, ALU.mult)
         tt(A("wf"), A("wf"), A("iw"), ALU.add)
         tt(A("wf"), A("wf"), A("slw"), ALU.max)
         for b in range(4):
             ts(A("wu", 20 * b, 20 * b + 20), A("wf"), 4.0, ALU.mult, float(b), ALU.add)
 
+    def gh2(b, h):
+        return A("gh", 512 + 256 * b + 128 * h, 640 + 256 * b + 128 * h)
+
+    cp(A("ptu"), A("ptw"))
+    for b in range(4):
+        act(gh2(b, 0), B4("at1", 0, 512, b), scale=0.5)
+    picks(0, "tv1", lambda b: gh2(b, 0))
     cp(A("adf", 8, 16), A("adw"))
     ts(A("cw"), A("cw"), q_, ALU.add)
     tt(A("cd", 0, 8), A("cw", 0, 8), A("adf", 8, 16), ALU.subtract)
@@ -413,41 +452,56 @@ def rank_program(g, core, T, topo):
     tt(A("no", 0, 8), A("no", 0, 8), A("cd", 0, 8), ALU.mult)
     tt(A("no", 0, 8), A("no", 0, 8), A("adf", 8, 16), ALU.add)
     cp(A("adu", 0, 8), A("no", 0, 8))
-    cp(A("ptu"), A("ptw"))
     for b in range(4):
         f = PL * b
         tt(B4("bt1", 0, 512, b), A("gh", 128 * b, 128 * b + 128), A("fg1", f + 320, f + 448), ALU.add, li=A("adu", 0, 8))
-
-    def gh2(b, h):
-        return A("gh", 512 + 256 * b + 128 * h, 640 + 256 * b + 128 * h)
-
-    for h, t in ((1, "bt1"), (0, "at1")):
+    for b in range(4):
+        act(gh2(b, 1), B4("bt1", 0, 512, b), scale=0.5)
+    picks(1, "tv1", lambda b: gh2(b, 1))
+    trial(0, "vl1", "fg1", "tv1", lambda b: gh2(b, 0))
+    act(A("t0s"), A("p5", 0, 320))
+    trial(1, "vl1", "fg1", "tv1", lambda b: gh2(b, 1))
+    if far:
+        need(E, "arrx", 24)
         for b in range(4):
-            act(gh2(b, h), B4(t, 0, 512, b), scale=0.5)
-    trials("vl1", "fg1", lambda b: gh2(b, 0), lambda b: gh2(b, 1), A("ptu"))
+            mm("p%d" % b, 448, "qe", "se", 128 * b, "lcx", "lsx", 0)
+            unpack(b, "fgx", 448, "ghx")
     slots(A("offu", 0, 8), 128)
     choose("more")
-    act(A("mm", 0, 320), A("more"), scale=BIG)
-    act(A("mm", 320, 640), A("more"), scale=-BIG, bias=BIG, func=AF.Identity)
-    tt(A("mm", 0, 320), A("mm", 0, 320), A("msk"), ALU.add)
-    tt(A("mm", 320, 640), A("mm", 320, 640), A("msk"), ALU.add)
-    ts(A("sx1", 320, 464), A("hb"), 32.0, ALU.subtract, 2.0 ** 80, ALU.mult)
+    if far:
+        need(V, "arrl", 8)
+        for b in range(4):
+            tt(B4("atx", 0, 512, b), A("fgx", 448 * b, 448 * b + 448), A("ghx", 128 * b, 128 * b + 128), ALU.add, li=A("llx"))
+        quant("qax", "sax", 0, 128, "atx", 0)
+    for c in range(2):
+        act(A("mks", L * c, L * c + L), A("more"), scale=2 * BIG * (1 - 2 * c), bias=-BIG * (1 - 2 * c), func=AF.Relu, li=A("order", 0, 21))
+    count(0, thB, A("accs", 1, 2))
+    act(A("opr", 320, 640), A("more", 0, 320), scale=128.0)
     ts(A("el", 2, 3), A("accs", 1, 2), 0.5, ALU.mult, addB2, ALU.add)
+    quant("qvv", "svv", 0, 128, "vs", 0)
     for b in range(4):
         act(A("fg2", PL * b + 320, PL * b + 576), A("gh", 512 + 256 * b, 768 + 256 * b))
-    parts_of_L(1, 128, "vl1")
+    if far:
+        parts_of_L("qax", "sax", 128, "vl1")
+    else:
+        need(E, "arr1", 16)
+        parts_of_L("lc1", "ls1", 128, "vl1")
     new_state("vl1", 128, "xt2")
     quant("qx", "sx", 0, 320, "xt2", 0)
     mm("p4", 320, "qur", "sur", 0, "qx", "sx", 0)
     for b in range(4):
         mm("p%d" % b, 320, "qe", "se", 128 * b, "qx", "sx", 0)
+    ts(A("pt2f"), A("mw"), 128.0, ALU.mult)
+    tt(A("pt2f"), A("pt2f"), A("ptw"), ALU.add)
+    cp(A("ptu"), A("pt2f"))
+    ts(A("adf", 0, 8), A("cw", 0, 8), 128.0, ALU.add)
+    tt(A("cd"), A("cw"), A("adf"), ALU.subtract)
 
-    tt(A("sx1", 0, 320), A("p4", 0, 320), A("mm", 320, 640), ALU.subtract)
-    tt(A("sx0", 0, 320), A("p4", 0, 320), A("mm", 0, 320), ALU.subtract)
-    act(A("ss1"), A("sx1"), li=A("order", 0, 21))
-    cp(A("ss0"), A("sx0"), li=A("order", 0, 21))
+    tt(A("sx0", 0, 320), A("p4", 0, 320), A("msk"), ALU.subtract)
+    for c in range(2):
+        tt(A("ss%d" % c), A("sx0"), A("mks", L * c, L * c + L), ALU.subtract, li=A("order", 0, 21))
     for b in range(4):
-        act(A("fg2", PL * b, PL * b + 320), A("p%d" % b, 0, 320), scale=0.5)
+        act(A("fg2", PL * b, PL * b + 320), A("p%d" % b, 0, 320))
     argmax(0)
     argmax(1)
     tt(A("off2"), A("s2"), A("kk"), ALU.add, li=A("el", 2, 3))
@@ -458,39 +512,42 @@ def rank_program(g, core, T, topo):
         f = PL * b
         tt(B4("g3", 0, 1024, b), A("fg2", f, f + 576), A("gh", 512 + 256 * b, 768 + 256 * b), ALU.add, li=A("offv"))
     quant("qg", "sg3", 0, 256, "g3", 0)
-    send(2, "qg", "sg3", 256)
+    send("2", "qg", "sg3", 256)
+    iota(A("sl"), [[0, 576]], 0, 0)
 
-    ts(A("adf", 0, 8), A("cw", 0, 8), 128.0, ALU.add)
-    tt(A("cd"), A("cw"), A("adf"), ALU.subtract)
+    def half2(h):
+        for b in range(4):
+            act(A("ab2", 512 * b + 256 * h, 512 * b + 256 * h + 256), B4("g3", 1024 * h, 1024 * h + 1024, b), scale=0.5)
+
+    def ab2(h):
+        return lambda b: A("ab2", 512 * b + 256 * h, 512 * b + 256 * h + 256)
+
+    half2(0)
+    picks(0, "tv2", ab2(0))
     ts(A("no"), A("off2"), 319.5, ALU.is_ge)
     tt(A("no"), A("no"), A("cd"), ALU.mult)
     tt(A("no"), A("no"), A("adf"), ALU.add)
     cp(A("adu"), A("no"))
-    ts(A("pt2f"), A("mw"), 128.0, ALU.mult)
-    tt(A("pt2f"), A("pt2f"), A("ptw"), ALU.add)
-    cp(A("ptu"), A("pt2f"))
     for b in range(4):
         f = PL * b
         tt(B4("g3", 1024, 2048, b), A("gh", 512 + 256 * b, 768 + 256 * b), A("fg2", f + 320, f + 576), ALU.add, li=A("adu"))
-    for h in (1, 0):
-        for b in range(4):
-            act(A("ab2", 512 * b + 256 * h, 512 * b + 256 * h + 256), B4("g3", 1024 * h, 1024 * h + 1024, b), scale=0.5)
-    trials("vl2", "fg2", lambda b: A("ab2", 512 * b, 512 * b + 256), lambda b: A("ab2", 512 * b + 256, 512 * b + 512), A("ptu"))
-    act(A("opr", 320, 640), A("more"), scale=128.0)
+    half2(1)
+    picks(1, "tv2", ab2(1))
+    trial(0, "vl2", "fg2", "tv2", ab2(0))
+    act(A("t0s"), A("p5", 0, 320))
+    trial(1, "vl2", "fg2", "tv2", ab2(1))
     slots(A("offv"), 256)
     choose("mor2")
+    act(A("opr", 0, 320), A("mor2"), scale=256.0)
     quant("qg", "sg3", 256, 512, "g3", 1024)
-    quant("qvv", "svv", 0, 128, "vs", 0)
     mm("p7", 512, "qvv", "svv", 0, "qg", "sg3", 0)
     act(A("zs", 0, 512), A("p7"))
     dma(Y, T.z[:, :], T.zs[:, 0:512], "d_out1", ins=[A("zs", 0, 512)[1]])
     cp(A("pti"), A("ptr"), li=A("clu"))
-    tt(A("opr", 0, 320), A("opr", 320, 640), A("pti"), ALU.add)
-    act(A("pti"), A("mor2"), scale=256.0)
-    tt(A("opr", 0, 320), A("opr", 0, 320), A("pti"), ALU.add)
-    dma(Y, T.op[:, :], T.opr[0:128:16, 0:320], "d_out1", ins=[A("opr", 0, 320)[1]])
+    tt(A("opr", 320, 640), A("opr", 320, 640), A("pti"), ALU.add)
 
-    parts_of_L(2, 256, "vl2")
+    need(E, "arr2", 24 if far else 16)
+    parts_of_L("lc2", "ls2", 256, "vl2")
     new_state("vl2", 256, "xt3")
     quant("qx3", "sx3", 0, 320, "xt3", 0)
     mm("p4", 320, "qvv", "svv", 0, "qx3", "sx3", 0)
@@ -499,9 +556,11 @@ def rank_program(g, core, T, topo):
         dma(Y, T.osc[4 * k:4 * k + 4, :], T.sx3[32 * k:32 * k + 4, 0:320], "d_out1", ins=[A("sx3")[1]])
     act(A("zs", 512, 832), A("p4", 0, 320))
     dma(S, T.y[:, :], T.zs[:, 512:832], "d_out2", ins=[A("zs", 512, 832)[1]])
+    tt(A("opr", 0, 320), A("opr", 0, 320), A("opr", 320, 640), ALU.add)
+    dma(Y, T.op[:, :], T.opr[0:128:16, 0:320], "d_out1", ins=[A("opr", 0, 320)[1]])
 
     for q in (V, S, E, G):
         need(G, qsem[q], cnt[q])
     for s, n in (("d_ptw", 16), ("d_rep", 256), ("d_x", 16), ("d_k", 16), ("d_u", 16), ("d_v", 16), ("d_w", 16), ("d_ws", 16), ("d_ad", 16), ("d_out1", 112), ("d_out2", 16),
-                 ("loc", sent[0]), ("arr1", narr), ("arr2", narr)):
+                 ("loc", sent[0])) + ((("arrx", 24), ("arrl", 8), ("arr2", 24)) if far else (("arr1", 16), ("arr2", 16))):
         need(G, s, n)

from concourse.bass import DstId, RemoteDMATransfer
from concourse.mybir import dt, AluOpType as ALU, AxisListType, ActivationFunctionType as AF

F4, BF, I4, U2, C8, S8 = "float32", "bfloat16", "int32", "uint16", "float8_e4m3fn_x4", "uint8"
PL, L, LS = 576, 336, 328
NV = 5
NS = 20 - NV
BIG = 2.0 ** 86


def _sb(n, d):
    return ("sbuf", [128, n], d)


SCRATCH = {
    "xs": _sb(1280, BF), "ks": _sb(512, BF), "us": _sb(512, BF), "vs": _sb(512, BF),
    "qxk": _sb(448, C8), "sxk": _sb(448, S8), "qu": _sb(128, C8), "su": _sb(128, S8), "qur": _sb(128, C8), "sur": _sb(128, S8),
    "qvv": _sb(128, C8), "svv": _sb(128, S8), "qw": _sb(512, C8), "sw": _sb(512, S8),
    "et": _sb(2048, BF), "ones": _sb(128, BF), "qe": _sb(512, C8), "se": _sb(512, S8),
    "ptw": _sb(20, I4), "ptr": _sb(320, I4), "adw": _sb(8, I4), "h16": _sb(320, I4), "lo": _sb(320, I4), "hw16": _sb(20, I4),
    "pidx": _sb(4, I4), "dgi": _sb(16, I4), "iq": _sb(320, F4), "vk": _sb(L, F4), "dg": _sb(L, F4), "tb": _sb(L, F4), "hb": _sb(144, F4), "cid": _sb(256, F4),
    "keyr": _sb(320, F4), "junk": _sb(1920, BF), "cmpv": _sb(960, BF),
    "vv": _sb(L, F4), "dgt": _sb(L, F4), "dgs": _sb(L, F4), "inc": _sb(LS, F4), "d0": _sb(LS, F4), "msk": _sb(320, F4), "mks": _sb(2 * L, F4),
    "sx0": _sb(464, F4), "ss0": _sb(L, F4), "ss1": _sb(L, F4), "st0": _sb(L, F4), "st1": _sb(L, F4),
    "nr0": _sb(LS, F4), "nr1": _sb(LS, F4), "s2": _sb(2 * LS, F4), "offu": _sb(16, U2),
    "fg1": _sb(4 * PL, BF), "fg2": _sb(4 * PL, BF), "gh": _sb(1536, BF), "at1": _sb(512, BF), "bt1": _sb(512, BF), "g3": _sb(2048, BF), "ab2": _sb(2048, BF),
    "vl1": _sb(4 * 768, BF), "vl2": _sb(4 * 896, BF), "xt2": _sb(1280, BF), "xt3": _sb(1280, BF), "fgx": _sb(1792, BF), "ghx": _sb(512, BF), "atx": _sb(512, BF),
    "tv1": _sb(2560, BF), "tv2": _sb(2560, BF),
    "qa1": _sb(128, C8), "sa1": _sb(128, S8), "qax": _sb(128, C8), "sax": _sb(128, S8), "qg": _sb(512, C8), "sg3": _sb(512, S8), "qv": _sb(640, C8), "sv3": _sb(640, S8),
    "qx": _sb(320, C8), "sx": _sb(320, S8), "qx3": _sb(320, C8), "sx3": _sb(320, S8),
    "t0s": _sb(320, F4), "more": _sb(464, F4), "mor2": _sb(320, F4), "sl": _sb(576, F4), "pti": _sb(320, F4), "opr": _sb(640, F4), "zs": _sb(832, F4),
    "lcx": _sb(448, C8), "lsx": _sb(448, S8), "llx": _sb(8, U2), "lc1": _sb(128, C8), "ls1": _sb(128, S8), "lc2": _sb(256, C8), "ls2": _sb(256, S8),
    "rcx": _sb(224, C8), "rsx": _sb(448, S8), "rlx": _sb(8, U2), "rc2": _sb(128, C8), "rs2": _sb(256, S8),
}
ALIAS = {}


def _pack(base, dtype, parts):
    at = 0
    for n, w in parts:
        ALIAS[n] = (base, at, w)
        at += -(-w // 16) * 16
    SCRATCH[base] = _sb(at, dtype)


_pack("sm", F4, [("cst", 16), ("iw", 20), ("iw32", 20), ("clf", 22), ("uif", 8), ("vsrc", 16), ("kk", 16), ("cw", 16), ("dg16", 16), ("keyw", 20), ("hwf", 20), ("acc", 16), ("accs", 2),
                 ("cntv", 8), ("posa", 20), ("offf", 16), ("off2", 16), ("adf", 16), ("cd", 16), ("no", 16), ("pt2f", 20), ("mw", 20), ("slw", 20), ("wf", 20)])
_pack("ul", U2, [("clu", 20), ("uiu", 8), ("dgl", 22), ("plist", 22), ("el", 4), ("order", 22), ("offv", 16), ("adu", 16), ("ptu", 20), ("wu", 80)])
for _i in range(8):
    SCRATCH["p%d" % _i] = ("psum", [128, 512], F4)
_DS = ["d_ptw", "d_rep", "d_x", "d_k", "d_u", "d_v", "d_w", "d_ws", "d_ad", "d_out1", "d_out2"]
SEMAPHORES = ["qv_s", "qs_s", "qt_s", "qg_s", "arr1", "arr2", "arrx", "arrl", "rinx", "rinl", "rin2", "loc"] + _DS


def _bits(es):
    return sum(1 << e for e in es)


def _relays(src, dst, T, topo):
    if topo.may_write(src, dst):
        return []
    c = [d for d in topo.cores_of(src) if d != src and T.rank_of(d) is None and topo.may_write(d, dst)]
    a, b = [d for d in c if topo.die(d) == topo.die(src)], [d for d in c if topo.die(d) != topo.die(src)]
    return [d for p in zip(a, b) for d in p][:3]


def _hand_on(g, core, T, topo):
    sent = 0
    for r, src in enumerate(T.cores):
        dst = T.cores[(r + 1) % len(T.cores)]
        rel = _relays(src, dst, T, topo)
        if core not in rel:
            continue
        j = rel.index(core)
        rid, pid = topo.addr(dst, core)
        m = _bits(topo.engines(core, dst)[:8])

        def piece(tag, n):
            g.wait_ge(T.sem["rin" + tag], 8)
            if j < 2:
                h = n // 2
                o, i = T["lc" + tag][:, h * j:h * j + h].bitcast(dt.uint8), T["rc" + tag][:, 0:h].bitcast(dt.uint8)
            else:
                o, i = T["ls" + tag][:, 0:n], T["rs" + tag][:, 0:n]
            g.remote_dma(o, i, T.sem["arr" + tag], T.sem["loc"], pid, rid, m)
        piece("x", 448)
        if j == 2:
            g.wait_ge(T.sem["rinl"], 8)
            g.remote_dma(T.llx[:, 0:8], T.rlx[:, 0:8], T.sem["arrl"], T.sem["loc"], pid, rid, m)
            sent += 8
        piece("2", 256)
        sent += 16
    if sent:
        g.wait_ge(T.sem["loc"], sent)


def rank_program(g, core, T, topo):
    rank = T.rank_of(core)
    if rank is None:
        _hand_on(g, core, T, topo)
        return
    nranks = len(T.cores)
    prev, nxt = T.cores[(rank - 1) % nranks], T.cores[(rank + 1) % nranks]
    rel, far = _relays(core, nxt, T, topo), bool(_relays(prev, core, T, topo))
    V, S, E, G, Y = "v", "s", "t", "g", "y"
    eng = {V: g.vector, S: g.scalar, E: g.tensor, G: g, Y: g.sync}
    qsem = {V: "qv_s", S: "qs_s", E: "qt_s", G: "qg_s"}
    cnt = {V: 0, S: 0, E: 0, G: 0}
    seen = {q: {} for q in eng}
    hist = {}

    def need(q, sem, n):
        if seen[q].get(sem, 0) < n:
            eng[q].wait_ge(T.sem[sem], n)
            seen[q][sem] = n

    def track(q, outs, ins, token=None):
        acc = [(r, True) for r in outs] + [(r, False) for r in ins]
        waits = {}
        for (name, lo, hi, ph), w in acc:
            ps = name[0] == "p" and name[1:].isdigit()
            for (l2, h2, p2, w2, tok, q2) in hist.get(name, []):
                if l2 < hi and lo < h2 and (ph is None or p2 is None or ph == p2) and (w or w2 or (ps and q2 != q)):
                    waits[tok[0]] = max(waits.get(tok[0], 0), tok[1])
        for s, n in waits.items():
            need(q, s, n)
        if token is None:
            cnt[q] += 1
            token = (qsem[q], cnt[q])
        for (name, lo, hi, ph), w in acc:
            h = hist.setdefault(name, [])
            if w and ph is None:
                h[:] = [e for e in h if not (lo <= e[0] and e[1] <= hi)]
            h.append((lo, hi, ph, w, token, q))
        return token

    def run(q, outs, ins, f):
        track(q, [o[1] for o in outs], [i[1] for i in ins])
        f().then_inc(T.sem[qsem[q]], 1)

    def A(name, lo=0, hi=None):
        if name in ALIAS:
            name, at, w = ALIAS[name]
            lo, hi = at + lo, at + (w if hi is None else hi)
        hi = SCRATCH[name][1][1] if hi is None else hi
        return (T[name][:, lo:hi], (name, lo, hi, None))

    def B4(name, lo, hi, b):
        return (T[name][:, lo + b:hi:4], (name, lo, hi, b))

    def St(name, hi, lo=15, step=16):
        return (T[name][:, lo:hi:step], (name, 0, hi, None))

    def ind(a, li):
        return a[0] if li is None else a[0].indirect(li[0])

    def opt(*xs):
        return [x for x in xs if isinstance(x, tuple)]

    def val(x):
        return x[0] if isinstance(x, tuple) else x

    def tt(o, a, b, op, li=None):
        run(V, [o], [a, b] + opt(li), lambda: g.vector.tensor_tensor(o[0], ind(a, li), b[0], op))

    def ts(o, a, s1, op0, s2=None, op1=None, li=None):
        if op1 is None:
            run(V, [o], [a] + opt(li, s1), lambda: g.vector.tensor_scalar(o[0], ind(a, li), val(s1), None, op0))
        else:
            run(V, [o], [a] + opt(li, s1, s2), lambda: g.vector.tensor_scalar(o[0], ind(a, li), val(s1), val(s2), op0, op1))

    def cp(o, a, li=None):
        run(V, [o], [a] + opt(li), lambda: g.vector.tensor_copy(o[0], ind(a, li)))

    def scatter(o, li, a):
        run(V, [o], [a, li], lambda: g.vector.tensor_copy(o[0].indirect(li[0]), a[0]))

    def fill(o, c):
        run(V, [o], [], lambda: g.vector.memset(o[0], c))

    def scan(o, a, b, init, op0, op1):
        run(V, [o], [a, b], lambda: g.vector.tensor_tensor_scan(o[0], a[0], b[0], init, op0, op1))

    def act(o, a, scale=1.0, bias=0.0, func=None, li=None, accum=None):
        fn = AF.Copy if func is None else func

        def f():
            kw = {}
            if isinstance(bias, tuple) or bias != 0.0:
                kw["bias"] = val(bias)
            if scale != 1.0:
                kw["scale"] = scale
            if accum is not None:
                kw["accum_out"] = accum[0]
            return g.scalar.activation(o[0], ind(a, li), fn, **kw)
        run(S, [o] + opt(accum), [a] + opt(li, bias), f)

    def iota(o, pattern, base, cm):
        def f():
            if SCRATCH[o[1][0]][2] == I4:
                return g.iota(o[0], pattern, base, cm)
            return g.iota(o[0], pattern, base, cm, allow_small_or_imprecise_dtypes=True)
        run(G, [o], [], f)

    def quant(q, s, lo, hi, t, tlo):
        a, b, c = A(q, lo, hi), A(s, lo, hi), A(t, tlo, tlo + 4 * (hi - lo))
        run(V, [a, b], [c], lambda: g.vector.quantize_mx(a[0], b[0], c[0]))

    def mm(p, n, wq, ws, wlo, xq, xs, xlo):
        o = A(p, 0, n)
        w, w2, x, x2 = A(wq, wlo, wlo + 128), A(ws, wlo, wlo + 128), A(xq, xlo, xlo + n), A(xs, xlo, xlo + n)
        run(E, [o], [w, w2, x, x2], lambda: g.tensor.matmul_mx(o[0], w[0], w2[0], x[0], x2[0], True, True))

    def dma(q, out, in_, sem, n=16, outs=(), ins=()):
        track(q, list(outs), list(ins), token=(sem, n))
        eng[q].dma_start(out, in_).then_inc(T.sem[sem], 16)

    def load(q, name, src, sem):
        a = A(name)
        dma(q, a[0], src, sem, outs=[a[1]])

    sent = [0]

    def remote(out, src, reg, sem, dst, es):
        track(G, [], [reg], token=("loc", 0))
        rid, pid = topo.addr(dst, core)
        g.remote_dma(out, src, T.sem[sem], T.sem["loc"], pid, rid, _bits(es))
        sent[0] += len(es)

    def send(tag, qn, sn, n):
        c, s = A(qn, 0, n), A(sn, 0, n)
        if not rel:
            es = topo.engines(core, nxt)
            remote(T["lc" + tag][:, 0:n].bitcast(dt.uint8), c[0].bitcast(dt.uint8), c[1], "arr" + tag, nxt, es[0:8])
            remote(T["ls" + tag][:, 0:n], s[0], s[1], "arr" + tag, nxt, es[8:16])
            return
        track(G, [], [c[1]], token=("loc", 0))
        h, tr = n // 2, []
        for j in range(2):
            rid, pid = topo.addr(rel[j], core)
            es = topo.engines(core, rel[j])[8 * j:8 * j + 8]
            tr.append(RemoteDMATransfer(dst_ids=[DstId(rid=rid, pnc=pid)], dma_engine_mask=_bits(es), remote_sem=T.sem["rin" + tag],
                                        src=T[qn][:, h * j:h * j + h].bitcast(dt.uint8), dst=T["rc" + tag][:, 0:h].bitcast(dt.uint8)))
            sent[0] += len(es)
        g.remote_dma_fused(tr, local_sem=T.sem["loc"])
        remote(T["rs" + tag][:, 0:n], s[0], s[1], "rin" + tag, rel[2], topo.engines(core, rel[2])[0:8])

    load(S, "ptw", T.pt[:, :], "d_ptw")
    for q in range(16):
        dma(S if q % 2 else Y, T.ptr[q:128:16, :], T.pt[:, :], "d_rep", n=256)
    hist["ptr"] = [(0, 320, None, True, ("d_rep", 256), "dma")]
    load(Y, "us", T.u[:, :], "d_u")
    load(S, "xs", T.x[:, :], "d_x")
    load(Y, "ks", T.k[:, :], "d_k")
    dma(Y, T.qw[:, 0:512].bitcast(dt.uint8), T.wc[:, :], "d_w", outs=[("qw", 0, 512, None)])
    load(Y, "sw", T.ws[:, :], "d_ws")
    load(Y, "adw", T.ad[:, :], "d_ad")
    load(Y, "vs", T.v[:, :], "d_v")

    iota(A("pidx", 0, 1), [[1, 1]], 0, 1)
    iota(A("iq"), [[1, 16], [16, 20]], 0, 0)
    iota(A("iw"), [[16, 20]], 0, 0)
    iota(A("clf"), [[1, 22]], 0, 0)
    iota(A("dgi"), [[1, 16]], 128, -1)
    iota(A("uif"), [[16, 8]], 0, 0)
    iota(A("kk"), [[0, 2], [16, 8]], 336, 0)
    iota(A("hb"), [[1, 9], [0, 16]], 0, 0)
    fill(A("ones"), 0.5)
    fill(A("et"), 0.0)
    for b in range(4):
        o, i = B4("et", 512 * b, 512 * b + 512, b), A("ones")
        run(G, [o], [i], lambda: g.affine_select(o[0], i[0], [[-1, 128]], ALU.is_equal, 0.0, 0, 1))
    iota(A("vk", 0, 320), [[1, 320]], 0, 0)
    iota(A("vsrc"), [[16, 16]], 336, 0)
    iota(A("tb"), [[0, L]], 0, 0)
    iota(St("tb", L, 0), [[0, 21]], 2 ** 22, 0)
    iota(A("st0", 0, 8), [[0, 8]], 0, 0)
    iota(A("st1", 0, 8), [[0, 8]], 0, 0)
    iota(A("cw"), [[16, 16]], 0, 0)

    pf, q_, q8, thA, thB, addA, addB, addB2, tmpc, q20 = [A("cst", j, j + 1) for j in range(10)]
    qi, q8i = A("pidx", 1, 2), A("pidx", 2, 3)
    act(A("iq"), A("iq"), scale=0.03125)
    ts(qi, A("pidx", 0, 1), 15, ALU.bitwise_and)
    ts(q8i, A("pidx", 0, 1), 7, ALU.bitwise_and)
    cp(q_, qi)
    cp(q8, q8i)
    ts(A("dgl"), A("clf"), 0.0, ALU.mult, q_, ALU.add)
    ts(A("dgi"), A("dgi"), 15, ALU.bitwise_and)
    ts(A("dg16"), A("dgi"), 0.0, ALU.not_equal, 2.0 ** 20, ALU.mult)
    ts(A("iw"), A("iw"), q_, ALU.add)
    ts(A("iw32"), A("iw"), 0.03125, ALU.mult)
    ts(thA, q_, 16.0, ALU.mult, 14.0, ALU.add)
    ts(thB, q8, 16.0, ALU.mult, 14.0, ALU.add)
    ts(tmpc, q_, 15.0, ALU.is_equal, -336.0, ALU.mult)
    ts(addA, q_, tmpc, ALU.add, 161.0, ALU.add)
    ts(addB, q8, 160.0, ALU.add)
    ts(pf, q_, 8.0, ALU.is_ge, float(LS), ALU.mult)
    tt(addB2, addB, pf, ALU.add)
    ts(q20, q_, 20.0, ALU.mult)
    cp(A("uiu"), A("uif"))
    ts(A("clu"), A("clf", 0, 20), q20, ALU.add)
    act(A("dg"), A("dg16"), li=A("dgl", 0, 21))
    act(A("kk"), A("kk"), bias=q_, func=AF.Identity)
    act(A("sx0", 320, 464), A("hb"), scale=2.0 ** 80, bias=-32 * 2.0 ** 80, func=AF.Identity)
    act(A("more", 320, 464), A("hb"), scale=0.0, bias=0.5, func=AF.Identity)

    ts(A("h16"), A("ptr"), 0x70, ALU.bitwise_and)
    ts(A("hw16"), A("ptw"), 0x70, ALU.bitwise_and)
    tt(A("keyr"), A("h16"), A("iq"), ALU.add)
    tt(A("keyw"), A("hw16"), A("iw32"), ALU.add)

    def count(k, bias, out):
        j = 320 * (k % 6)
        act(A("junk", j, j + 320), A("keyr"), scale=-1.0, bias=bias, func=AF.Sign, accum=out)

    for k in range(NS):
        count(k, A("keyw", k, k + 1), A("acc", k, k + 1))
    count(NS, thA, A("accs", 0, 1))

    def lane(j):
        o, c = A("cntv", j, j + 1), A("cmpv", 320 * (j % 3), 320 * (j % 3) + 320)
        ts(c, A("keyr"), A("keyw", NS + j, NS + j + 1), ALU.is_lt)
        run(V, [o], [c], lambda: g.vector.tensor_reduce(o[0], c[0], AxisListType.X, ALU.add))

    lane(0)
    lane(1)
    quant("qxk", "sxk", 0, 320, "xs", 0)
    quant("qxk", "sxk", 320, 448, "ks", 0)
    if rel:
        send("x", "qxk", "sxk", 448)
    iota(A("cid"), [[1, 256]], 640, 0)
    iota(A("sl", 0, 448), [[0, 448]], 0, 0)
    quant("qu", "su", 0, 128, "us", 0)
    o1, i1, l1 = A("qur"), A("qu"), A("uiu")
    run(V, [o1], [i1, l1], lambda: g.vector.tensor_copy(T.qur[:, 0:128].bitcast(dt.uint32), T.qu[:, 0:128].bitcast(dt.uint32).indirect(l1[0])))
    cp(A("sur"), A("su"), li=l1)
    mm("p4", 320, "qur", "sur", 0, "qxk", "sxk", 0)
    quant("qe", "se", 0, 512, "et", 0)
    for b in range(4):
        mm("p%d" % b, 448, "qe", "se", 128 * b, "qxk", "sxk", 0)
    for j in range(2, NV):
        lane(j)
    ts(A("lo"), A("ptr"), 15, ALU.bitwise_and)
    ts(A("msk"), A("lo"), q_, ALU.not_equal, BIG, ALU.mult, li=A("clu"))
    ts(A("vk", 320, 336), A("vsrc"), 448.0, ALU.min, q_, ALU.add)
    ts(A("vk", 335, 336), q_, 320.0, ALU.add)
    ts(A("hwf"), A("hw16"), 0.0625, ALU.mult)
    tt(A("sx0", 0, 320), A("p4", 0, 320), A("msk"), ALU.subtract)
    ts(A("posa", NS, 20), A("cntv", 0, NV), 1.0, ALU.add)
    ts(A("posa", 0, NS), A("acc", 0, NS), 0.5, ALU.mult, 160.5, ALU.add)
    tt(A("posa"), A("posa"), A("hwf"), ALU.add)
    cp(A("plist", 0, 20), A("posa"))
    ts(A("plist", 20, 21), A("accs", 0, 1), 0.5, ALU.mult, addA, ALU.add)
    scatter(A("vv"), A("plist", 0, 21), A("vk"))

    def diag(out, src, n):
        tt(A("dgt", 0, n), src, A("dg", 0, n), ALU.add)
        scan(A("dgs", 0, n), A("tb", 0, n), A("dgt", 0, n), 2.0 ** 22, ALU.max, ALU.min)
        cp(out, St("dgs", n))

    def unpack(b, fg, w, gh):
        act(A(fg, w * b, w * b + 448), A("p%d" % b, 0, 448))
        act(A(gh, 128 * b, 128 * b + 128), A("p%d" % b, 320, 448))

    unpack(0, "fg1", PL, "gh")
    unpack(1, "fg1", PL, "gh")
    diag(A("order", 0, 21), A("vv"), L)
    act(A("d0"), A("vv", 0, LS), scale=-2.0 ** 88, bias=319.5 * 2.0 ** 88, func=AF.Identity)
    act(A("ss0"), A("sx0"), li=A("order", 0, 21))
    for b in range(2, 4):
        unpack(b, "fg1", PL, "gh")
    tt(A("inc"), A("vv", 0, LS), A("vv", 1, LS + 1), ALU.subtract)
    ts(A("el", 0, 1), A("accs", 0, 1), 0.5, ALU.mult, addB, ALU.add)

    def argmax(c):
        scan(A("st%d" % c, 8, L), A("d0"), A("ss%d" % c, 0, LS), -BIG, ALU.min, ALU.max)
        tt(A("nr%d" % c), A("st%d" % c, 8, L), A("st%d" % c, 7, L - 1), ALU.is_equal)
        scan(A("s2", LS * c, LS * c + LS), A("nr%d" % c), A("inc"), 0.0, ALU.mult, ALU.add)

    argmax(0)
    tt(A("offf"), A("s2", 0, LS), A("kk"), ALU.add, li=A("el", 0, 1))
    cp(A("offu", 0, 8), A("offf", 0, 8))
    if rel:
        r = A("offu", 0, 8)
        remote(T.rlx[:, 0:8], r[0], r[1], "rinl", rel[2], topo.engines(core, rel[2])[0:8])
    for b in range(4):
        f = PL * b
        tt(B4("at1", 0, 512, b), A("fg1", f, f + 448), A("gh", 128 * b, 128 * b + 128), ALU.add, li=A("offu", 0, 8))
    if not rel:
        quant("qa1", "sa1", 0, 128, "at1", 0)
        send("1", "qa1", "sa1", 128)

    def parts_of_L(qn, sn, M, vl):
        for b in range(4):
            mm("p%d" % b, M, "qw", "sw", 128 * b, qn, sn, 0)
        for b in range(4):
            o, i = B4(vl, 2560, 2560 + 4 * M, b), A("p%d" % b, 0, M)
            if b % 2:
                ts(o, i, 0.03125, ALU.mult)
            else:
                act(o, i, scale=0.03125)

    def new_state(vl, M, xt):
        for b in (0, 2, 1, 3):
            o, i, li = B4(xt, 0, 1280, b), A(vl, 0, 2560 + 4 * M), A("wu", 20 * b, 20 * b + 20)
            if b % 2:
                act(o, i, li=li)
            else:
                cp(o, i, li=li)

    def slots(offu, M):
        scatter(A("sl", 0, 320 + M), offu, A("cid", 0, M))
        diag(A("slw"), A("sl", 0, 320), 320)

    own = (1, 2)

    def picks(h, tv, win):
        for b in range(own[h], 4):
            act(A(tv, 1280 * h + 320 * b, 1280 * h + 320 * b + 320), win(b), li=A("ptu"))

    def trial(h, vl, fg, tv, win):
        for b in range(4):
            o = B4(vl, 1280 * h, 1280 * h + 1280, b)
            if b < own[h]:
                tt(o, win(b), A(fg, PL * b, PL * b + 320), ALU.add, li=A("ptu"))
            else:
                tt(o, A("p%d" % b, 0, 320), A(tv, 1280 * h + 320 * b, 1280 * h + 320 * b + 320), ALU.add)
        quant("qv", "sv3", 320 * h, 320 * h + 320, vl, 1280 * h)
        mm("p%d" % (5 + h), 320, "qur", "sur", 0, "qv", "sv3", 320 * h)

    def choose(more):
        tt(A(more, 0, 320), A("p6", 0, 320), A("t0s"), ALU.is_gt)
        diag(A("mw"), A(more, 0, 320), 320)
        ts(A("wf"), A("mw"), 320.0, ALU.mult)
        tt(A("wf"), A("wf"), A("iw"), ALU.add)
        tt(A("wf"), A("wf"), A("slw"), ALU.max)
        for b in range(4):
            ts(A("wu", 20 * b, 20 * b + 20), A("wf"), 4.0, ALU.mult, float(b), ALU.add)

    def gh2(b, h):
        return A("gh", 512 + 256 * b + 128 * h, 640 + 256 * b + 128 * h)

    cp(A("ptu"), A("ptw"))
    for b in range(4):
        act(gh2(b, 0), B4("at1", 0, 512, b), scale=0.5)
    picks(0, "tv1", lambda b: gh2(b, 0))
    cp(A("adf", 8, 16), A("adw"))
    ts(A("cw"), A("cw"), q_, ALU.add)
    tt(A("cd", 0, 8), A("cw", 0, 8), A("adf", 8, 16), ALU.subtract)
    ts(A("no", 0, 8), A("offf", 0, 8), 319.5, ALU.is_ge)
    tt(A("no", 0, 8), A("no", 0, 8), A("cd", 0, 8), ALU.mult)
    tt(A("no", 0, 8), A("no", 0, 8), A("adf", 8, 16), ALU.add)
    cp(A("adu", 0, 8), A("no", 0, 8))
    for b in range(4):
        f = PL * b
        tt(B4("bt1", 0, 512, b), A("gh", 128 * b, 128 * b + 128), A("fg1", f + 320, f + 448), ALU.add, li=A("adu", 0, 8))
    for b in range(4):
        act(gh2(b, 1), B4("bt1", 0, 512, b), scale=0.5)
    picks(1, "tv1", lambda b: gh2(b, 1))
    trial(0, "vl1", "fg1", "tv1", lambda b: gh2(b, 0))
    act(A("t0s"), A("p5", 0, 320))
    trial(1, "vl1", "fg1", "tv1", lambda b: gh2(b, 1))
    if far:
        need(E, "arrx", 24)
        for b in range(4):
            mm("p%d" % b, 448, "qe", "se", 128 * b, "lcx", "lsx", 0)
            unpack(b, "fgx", 448, "ghx")
    slots(A("offu", 0, 8), 128)
    choose("more")
    if far:
        need(V, "arrl", 8)
        for b in range(4):
            tt(B4("atx", 0, 512, b), A("fgx", 448 * b, 448 * b + 448), A("ghx", 128 * b, 128 * b + 128), ALU.add, li=A("llx"))
        quant("qax", "sax", 0, 128, "atx", 0)
    for c in range(2):
        act(A("mks", L * c, L * c + L), A("more"), scale=2 * BIG * (1 - 2 * c), bias=-BIG * (1 - 2 * c), func=AF.Relu, li=A("order", 0, 21))
    count(0, thB, A("accs", 1, 2))
    act(A("opr", 320, 640), A("more", 0, 320), scale=128.0)
    ts(A("el", 2, 3), A("accs", 1, 2), 0.5, ALU.mult, addB2, ALU.add)
    quant("qvv", "svv", 0, 128, "vs", 0)
    for b in range(4):
        act(A("fg2", PL * b + 320, PL * b + 576), A("gh", 512 + 256 * b, 768 + 256 * b))
    if far:
        parts_of_L("qax", "sax", 128, "vl1")
    else:
        need(E, "arr1", 16)
        parts_of_L("lc1", "ls1", 128, "vl1")
    new_state("vl1", 128, "xt2")
    quant("qx", "sx", 0, 320, "xt2", 0)
    mm("p4", 320, "qur", "sur", 0, "qx", "sx", 0)
    for b in range(4):
        mm("p%d" % b, 320, "qe", "se", 128 * b, "qx", "sx", 0)
    ts(A("pt2f"), A("mw"), 128.0, ALU.mult)
    tt(A("pt2f"), A("pt2f"), A("ptw"), ALU.add)
    cp(A("ptu"), A("pt2f"))
    ts(A("adf", 0, 8), A("cw", 0, 8), 128.0, ALU.add)
    tt(A("cd"), A("cw"), A("adf"), ALU.subtract)

    tt(A("sx0", 0, 320), A("p4", 0, 320), A("msk"), ALU.subtract)
    for c in range(2):
        tt(A("ss%d" % c), A("sx0"), A("mks", L * c, L * c + L), ALU.subtract, li=A("order", 0, 21))
    for b in range(4):
        act(A("fg2", PL * b, PL * b + 320), A("p%d" % b, 0, 320))
    argmax(0)
    argmax(1)
    tt(A("off2"), A("s2"), A("kk"), ALU.add, li=A("el", 2, 3))
    ts(A("no", 0, 8), A("off2", 8, 16), 319.5, ALU.is_ge, 128.0, ALU.mult)
    tt(A("off2", 8, 16), A("off2", 8, 16), A("no", 0, 8), ALU.add)
    cp(A("offv"), A("off2"))
    for b in range(4):
        f = PL * b
        tt(B4("g3", 0, 1024, b), A("fg2", f, f + 576), A("gh", 512 + 256 * b, 768 + 256 * b), ALU.add, li=A("offv"))
    quant("qg", "sg3", 0, 256, "g3", 0)
    send("2", "qg", "sg3", 256)
    iota(A("sl"), [[0, 576]], 0, 0)

    def half2(h):
        for b in range(4):
            act(A("ab2", 512 * b + 256 * h, 512 * b + 256 * h + 256), B4("g3", 1024 * h, 1024 * h + 1024, b), scale=0.5)

    def ab2(h):
        return lambda b: A("ab2", 512 * b + 256 * h, 512 * b + 256 * h + 256)

    half2(0)
    picks(0, "tv2", ab2(0))
    ts(A("no"), A("off2"), 319.5, ALU.is_ge)
    tt(A("no"), A("no"), A("cd"), ALU.mult)
    tt(A("no"), A("no"), A("adf"), ALU.add)
    cp(A("adu"), A("no"))
    for b in range(4):
        f = PL * b
        tt(B4("g3", 1024, 2048, b), A("gh", 512 + 256 * b, 768 + 256 * b), A("fg2", f + 320, f + 576), ALU.add, li=A("adu"))
    half2(1)
    picks(1, "tv2", ab2(1))
    trial(0, "vl2", "fg2", "tv2", ab2(0))
    act(A("t0s"), A("p5", 0, 320))
    trial(1, "vl2", "fg2", "tv2", ab2(1))
    slots(A("offv"), 256)
    choose("mor2")
    act(A("opr", 0, 320), A("mor2"), scale=256.0)
    quant("qg", "sg3", 256, 512, "g3", 1024)
    mm("p7", 512, "qvv", "svv", 0, "qg", "sg3", 0)
    act(A("zs", 0, 512), A("p7"))
    dma(Y, T.z[:, :], T.zs[:, 0:512], "d_out1", ins=[A("zs", 0, 512)[1]])
    cp(A("pti"), A("ptr"), li=A("clu"))
    tt(A("opr", 320, 640), A("opr", 320, 640), A("pti"), ALU.add)

    need(E, "arr2", 24 if far else 16)
    parts_of_L("lc2", "ls2", 256, "vl2")
    new_state("vl2", 256, "xt3")
    quant("qx3", "sx3", 0, 320, "xt3", 0)
    mm("p4", 320, "qvv", "svv", 0, "qx3", "sx3", 0)
    dma(Y, T.oc[:, :], T.qx3[:, 0:320].bitcast(dt.uint8), "d_out1", ins=[A("qx3")[1]])
    for k in range(4):
        dma(Y, T.osc[4 * k:4 * k + 4, :], T.sx3[32 * k:32 * k + 4, 0:320], "d_out1", ins=[A("sx3")[1]])
    act(A("zs", 512, 832), A("p4", 0, 320))
    dma(S, T.y[:, :], T.zs[:, 512:832], "d_out2", ins=[A("zs", 512, 832)[1]])
    tt(A("opr", 0, 320), A("opr", 0, 320), A("opr", 320, 640), ALU.add)
    dma(Y, T.op[:, :], T.opr[0:128:16, 0:320], "d_out1", ins=[A("opr", 0, 320)[1]])

    for q in (V, S, E, G):
        need(G, qsem[q], cnt[q])
    for s, n in (("d_ptw", 16), ("d_rep", 256), ("d_x", 16), ("d_k", 16), ("d_u", 16), ("d_v", 16), ("d_w", 16), ("d_ws", 16), ("d_ad", 16), ("d_out1", 112), ("d_out2", 16),
                 ("loc", sent[0])) + ((("arrx", 24), ("arrl", 8), ("arr2", 24)) if far else (("arr1", 16), ("arr2", 16))):
        need(G, s, n)
